import numpy as np
import ml_dtypes


def mxq(x, axis, fmt="e4m3"):
    dtype, down = {"e4m3": (ml_dtypes.float8_e4m3fn, 7), "e5m2": (ml_dtypes.float8_e5m2, 14)}[fmt]
    v = np.moveaxis(np.asarray(x, np.float32).astype(ml_dtypes.bfloat16).astype(np.float64), axis, -1)
    blocks = v.reshape(v.shape[:-1] + (-1, 32))
    amax = np.abs(blocks).max(-1, keepdims=True)
    byte = np.maximum(np.where(amax > 0, np.frexp(amax)[1] - 1 + 127, 0) - down, 1)
    scale = np.exp2(byte - 127.0)
    codes = (blocks / scale).astype(np.float32).astype(dtype).astype(np.float64)
    return np.moveaxis((codes * scale).reshape(v.shape), -1, axis)


WIDE = False


def mx_kscale(k):
    if not WIDE:
        return np.ones(k)
    levels = np.array([10, -10, 5, -5, 0])
    if k % 512:
        return np.exp2(np.random.permutation(np.resize(levels, k // 32))).repeat(32)
    a = np.empty((k // 512, 16))
    for p in range(k // 512):
        a[p, :8] = np.random.permutation(np.resize(levels, 8))
        for g in range(8):
            far = levels[np.abs(levels - a[p, g]) >= 10]
            a[p, g + 8] = far[np.random.randint(len(far))]
    return np.exp2(a.ravel()).repeat(32)


BF16 = ml_dtypes.bfloat16


def bf(x):
    return np.asarray(x, np.float32).astype(BF16)


def f64(x):
    return np.asarray(x).astype(np.float64)


E2M1 = np.array([0.0, 0.5, 1.0, 1.5, 2.0, 3.0, 4.0, 6.0, -0.0, -0.5, -1.0, -1.5, -2.0, -3.0, -4.0, -6.0])


def pack_weight(w, fmt):
    k, n = w.shape
    w = f64(bf(w)).reshape(k // 32, 32, n)
    amax = np.abs(w).max(1)
    if fmt == "e4m3":
        byte = np.frexp(amax)[1] - 1 + 127 - 7
    else:
        mant, ex = np.frexp(amax / 6.0)
        byte = np.where(mant > 0.5, ex, ex - 1) + 127
    byte = np.clip(np.where(amax > 0, byte, 1), 1, 254)
    scaled = (w * np.exp2(127.0 - byte)[:, None, :]).reshape(k, n).astype(np.float32)
    by_word = np.ascontiguousarray(scaled.reshape(k // 512, 128, 4, n).transpose(0, 1, 3, 2))
    if fmt == "e4m3":
        words = by_word.astype(ml_dtypes.float8_e4m3fn).view(np.uint8)
    else:
        c = by_word.astype(ml_dtypes.float4_e2m1fn).view(np.uint8) & 0xF
        words = c[..., 0::2] | (c[..., 1::2] << 4)
    return np.ascontiguousarray(words), np.ascontiguousarray(byte.astype(np.uint8).reshape(k // 512, 16, n))


def unpack_weight(words, scales, fmt):
    g, p, n, _ = words.shape
    if fmt == "e4m3":
        vals = np.ascontiguousarray(words).view(ml_dtypes.float8_e4m3fn).astype(np.float64)
    else:
        nib = np.empty((g, p, n, 4), np.uint8)
        nib[..., 0::2] = words & 0xF
        nib[..., 1::2] = words >> 4
        vals = E2M1[nib]
    vals = vals * np.repeat(np.exp2(scales.astype(np.float64) - 127.0), 8, axis=1)[..., None]
    return vals.transpose(0, 1, 3, 2).reshape(g * 512, n)
def pack4(w):
    words, scales = pack_weight(w, "e2m1")
    return words.reshape(words.shape[0], 128, -1), scales


def unpack4(words, scales):
    return unpack_weight(words.reshape(words.shape[0], 128, -1, 2), scales, "e2m1")


def planes(Y):
    n, m = Y.shape
    b = f64(bf(Y)).reshape(n // 32, 32, m)
    amax = np.abs(b).max(1)
    byte = np.clip(np.where(amax > 0, np.frexp(amax)[1] - 1 + 127 - 7, 1), 1, 254)
    codes = (b * np.exp2(127.0 - byte)[:, None, :]).reshape(n, m).astype(np.float32).astype(ml_dtypes.float8_e4m3fn).view(np.uint8)
    words = codes.reshape(n // 512, 128, 4, m).transpose(0, 1, 3, 2)
    return np.ascontiguousarray(words), np.ascontiguousarray(byte.astype(np.uint8).reshape(n // 512, 16, m))


M, S, N = 1536, 1024, 2048

def setup_inputs():
    rn = np.random.randn
    s = mx_kscale(S)
    t = mx_kscale(S)
    propagator = rn(S, S) / np.sqrt(S) / s[:, None] * t[None, :]
    partition = rn(S, N) / np.sqrt(S) / t[:, None]
    propagator_words, propagator_scales = pack4(propagator)
    partition_words, partition_scales = pack4(partition)
    return {
        "states": bf(rn(M, S) * s[None, :]),
        "propagator_words": propagator_words,
        "propagator_scales": propagator_scales,
        "doses": bf(rn(M, S)),
        "uptake": bf(np.random.uniform(0.3, 0.9, S) * t),
        "partition_words": partition_words,
        "partition_scales": partition_scales,
        "inv_volume": bf(np.exp(0.7 * rn(N))),
        "inv_size": bf(np.exp(0.25 * rn(M))),
        "offset": bf(0.3 * rn(N)),
    }

def reference(states, propagator_words, propagator_scales, doses, uptake, partition_words, partition_scales, inv_volume, inv_size, offset):
    P = unpack4(propagator_words, propagator_scales)
    R = unpack4(partition_words, partition_scales)
    moved = mxq(f64(states), 1, "e4m3") @ P
    H = moved + f64(doses) * f64(uptake)[None, :]
    amount = mxq(H, 1, "e4m3") @ R
    y = amount * f64(inv_volume)[None, :] * f64(inv_size)[:, None] + f64(offset)[None, :]
    Y = y.T
    words, scales = planes(Y)
    return y, words, scales

@@ -1,0 +1,316 @@
+from contextlib import ExitStack
+
+import concourse.mybir as mybir
+from concourse.masks import make_identity
+
+M, S, N = 1536, 1024, 2048
+FLOPS = 2 * M * S * S + 2 * M * S * N
+
+F32 = mybir.dt.float32
+BF16 = mybir.dt.bfloat16
+I32 = mybir.dt.int32
+U32 = mybir.dt.uint32
+U8 = mybir.dt.uint8
+FP8X4 = mybir.dt.float8_e4m3fn_x4
+FP4X4 = mybir.dt.float4_e2m1fn_x4
+ALU = mybir.AluOpType
+ACT = mybir.ActivationFunctionType
+
+P = 128
+TILES = M // P
+KG = S // 512
+NG = N // 512
+BANK = 512
+POOL_COLS = 1408
+LAST_POOL_COLS = 768
+LOAD_GROUPS = [(0, 1), (1, 2), (2, 3), (3, 6), (6, 9), (9, 12)]
+WORD_GROUPS = [(0, 2), (2, 4), (4, 6), (6, 8), (8, 10), (10, 11), (11, 12)]
+SCALE_GROUPS = [(0, 10), (10, 12)]
+
+
+def group_of(groups, i):
+    return [grp for grp in groups if grp[0] <= i < grp[1]][0]
+
+
+def tile_pharmacokinetic_tissue_step_h1_kernel(
+    tc, states, propagator_words, propagator_scales, doses, uptake, partition_words, partition_scales,
+    inv_volume, inv_size, offset, out_0, out_1, out_2,
+):
+    nc = tc.nc
+    with ExitStack() as ctx:
+        keep = ctx.enter_context(tc.tile_pool(name="keep", bufs=1))
+        two = ctx.enter_context(tc.tile_pool(name="two", bufs=2))
+        three = ctx.enter_context(tc.tile_pool(name="three", bufs=3))
+        four = ctx.enter_context(tc.tile_pool(name="four", bufs=6))
+        ps_one = ctx.enter_context(tc.psum_pool(name="ps_one", bufs=1))
+        ps_two = ctx.enter_context(tc.psum_pool(name="ps_two", bufs=2))
+        ps_mx = ctx.enter_context(tc.psum_pool(name="ps_mx", bufs=4))
+        ctx.enter_context(tc.manual_schedule())
+
+        ident = keep.tile([P, P], F32, name="ident")
+        make_identity(nc, ident[:])
+        w_square = keep.tile([P, P], F32, name="w_square")
+        nc.gpsimd.memset(w_square[:], 0.0)
+
+        p_words = {}
+        p_scales = keep.tile([P, KG, S], U8, name="p_scales", align_bytes=64)
+        r_words = keep.tile([P, KG, 2 * N], U8, name="r_words", align_bytes=64)
+        r_scales = keep.tile([P, KG, N], U8, name="r_scales", align_bytes=64)
+        nc.vector.memset(p_scales[:].bitcast(I32), 0)
+        nc.vector.memset(r_scales[:].bitcast(I32), 0)
+
+        x_sb, d_sb = {}, {}
+
+        def load_rows(store, src, label, lo, hi):
+            rows = keep.tile([P, hi - lo, S], BF16, name="%s%d" % (label, lo))
+            nc.sync.dma_start(out=rows[:], in_=src[lo * P : hi * P, :].rearrange("(i p) k -> p i k", p=P))
+            for i in range(lo, hi):
+                store[i] = rows[:, i - lo, :]
+
+        def load_scale_rows(plane, src):
+            for q in range(4):
+                nc.sync.dma_start(
+                    out=plane[32 * q : 32 * q + 4, :, :].bitcast(I32),
+                    in_=src[:, 4 * q : 4 * q + 4, :].rearrange("g r n -> r g n").bitcast(I32),
+                )
+
+        u_raw = keep.tile([P, KG, 4], BF16, name="u_raw")
+        w_rows = keep.tile([TILES, P], BF16, name="w_rows")
+        v_bc = keep.tile([P, N], BF16, name="v_bc")
+        c_bc = keep.tile([P, N], BF16, name="c_bc")
+
+        def load_propagator(h):
+            p_words[h] = keep.tile([P, KG, 1024], U8, name="p_words%d" % h, align_bytes=64)
+            nc.sync.dma_start(
+                out=p_words[h][:].bitcast(I32),
+                in_=propagator_words[:, :, 1024 * h : 1024 * (h + 1)].rearrange("g p n -> p g n").bitcast(I32),
+            )
+
+        load_propagator(0)
+        load_rows(x_sb, states, "x", *LOAD_GROUPS[0])
+        load_scale_rows(p_scales, propagator_scales)
+        load_propagator(1)
+        load_rows(d_sb, doses, "d", *LOAD_GROUPS[0])
+        nc.sync.dma_start(out=u_raw[:], in_=uptake.rearrange("(g p t) -> p g t", g=KG, t=4))
+        nc.sync.dma_start(out=w_rows[:], in_=inv_size.rearrange("(i p) -> i p", p=P))
+        load_rows(x_sb, states, "x", *LOAD_GROUPS[1])
+        load_rows(d_sb, doses, "d", *LOAD_GROUPS[1])
+        nc.sync.dma_start(out=r_words[:].bitcast(I32), in_=partition_words.rearrange("g p n -> p g n").bitcast(I32))
+        load_scale_rows(r_scales, partition_scales)
+        nc.sync.dma_start(out=v_bc[:], in_=inv_volume.partition_broadcast(P))
+        nc.sync.dma_start(out=c_bc[:], in_=offset.partition_broadcast(P))
+        for grp in LOAD_GROUPS[2:]:
+            load_rows(x_sb, states, "x", *grp)
+            load_rows(d_sb, doses, "d", *grp)
+
+        u_col = keep.tile([P, KG * 4], F32, name="u_col")
+        nc.scalar.activation(out=u_col[:], in_=u_raw[:].rearrange("p g t -> p (g t)"), func=ACT.Copy)
+        w_col = keep.tile([P, TILES], F32, name="w_col")
+
+        p_words_sorted, p_scales_sorted = {}, {}
+
+        def sort_propagator(h):
+            words = keep.tile([P, KG, 1024], U8, name="p_words_sorted%d" % h, align_bytes=64)
+            scales = keep.tile([P, KG, 512], U8, name="p_scales_sorted%d" % h, align_bytes=64)
+            nc.vector.tensor_copy(
+                out=words[:].rearrange("p g (t m b) -> p g t m b", t=4, b=2),
+                in_=p_words[h][:].rearrange("p g (m t b) -> p g t m b", t=4, b=2),
+            )
+            nc.vector.tensor_copy(
+                out=scales[:].rearrange("p g (t m) -> p g t m", t=4),
+                in_=p_scales[:, :, 512 * h : 512 * (h + 1)].rearrange("p g (m t) -> p g t m", t=4),
+            )
+            p_words_sorted[h], p_scales_sorted[h] = words, scales
+
+        def spread_w():
+            nc.scalar.activation(out=w_square[0:TILES, :], in_=w_rows[:], func=ACT.Copy)
+            bank = ps_two.tile([P, BANK], F32, name="y_bank")
+            nc.tensor.transpose(bank[:, 0:P], w_square[:], ident[:])
+            nc.scalar.copy(out=w_col[:], in_=bank[:, 0:TILES])
+
+        x_grouped, x_q, du, h_grouped, h_q, y_sb, y_pairs, y_grouped = {}, {}, {}, {}, {}, {}, {}, {}
+        word_tiles, scale_tiles = {}, {}
+
+        def turn_pairs(bank, rows):
+            words = rows.bitcast(F32)
+            for g in range(KG):
+                for u in range(2):
+                    q = 2 * g + u
+                    nc.tensor.transpose(bank[:, q * P : (q + 1) * P], words[:, 256 * g + u : 256 * (g + 1) : 2], ident[:])
+
+        def interleave_out(dst, bank):
+            nc.scalar.copy(
+                out=dst.rearrange("p g m t -> p g (m t)").bitcast(F32).rearrange("p g (m u) -> p g m u", u=2),
+                in_=bank[:].rearrange("p (g u m) -> p g m u", g=2, u=2),
+            )
+
+        def turn_inputs(i):
+            x_bank = ps_one.tile([P, BANK], F32, name="x_bank")
+            turn_pairs(x_bank, x_sb[i])
+            x_grouped[i] = two.tile([P, KG, P, 4], BF16, name="x_grouped", align_bytes=64)
+            interleave_out(x_grouped[i][:], x_bank)
+            d_bank = ps_one.tile([P, BANK], F32, name="d_bank")
+            turn_pairs(d_bank, d_sb[i])
+            du[i] = three.tile([P, KG * 4, P], F32, name="du")
+            halves = d_bank[:].bitcast(BF16)
+            for g in range(KG):
+                for t in range(4):
+                    q = 2 * g + t // 2
+                    nc.scalar.activation(
+                        out=du[i][:, 4 * g + t, :],
+                        in_=halves[:, 256 * q + t % 2 : 256 * (q + 1) : 2],
+                        func=ACT.Copy,
+                        scale=u_col[:, 4 * g + t : 4 * g + t + 1],
+                    )
+
+        def quantize(src, label):
+            codes = three.tile([P, KG * P], U32, name=label + "_codes", align_bytes=64)
+            scales = three.tile([P, KG * P], U8, name=label + "_scales", align_bytes=64)
+            nc.vector.quantize_mx(out=codes[:].bitcast(FP8X4), scales=scales[:], in_=src[:].rearrange("p g m t -> p (g m t)"))
+            return codes, scales
+
+        def first_stage(i):
+            codes, scales = x_q[i]
+            h_grouped[i] = two.tile([P, KG, P, 4], BF16, name="h_grouped", align_bytes=64)
+            for h in range(KG):
+                bank = ps_mx.tile([P, BANK], F32, name="mx_bank")
+                for t in range(4):
+                    for g in range(KG):
+                        nc.tensor.matmul_mx(
+                            out=bank[:, t * P : (t + 1) * P],
+                            lhsT=p_words_sorted[h][:, g, 256 * t : 256 * (t + 1)].bitcast(FP4X4),
+                            lhsT_scale=p_scales_sorted[h][:, g, P * t : P * (t + 1)],
+                            rhs=codes[:, g * P : (g + 1) * P].bitcast(FP8X4),
+                            rhs_scale=scales[:, g * P : (g + 1) * P],
+                            start=(g == 0),
+                            stop=(g == KG - 1),
+                        )
+                nc.vector.tensor_tensor(
+                    out=h_grouped[i][:, h, :, :].rearrange("p (c i) t -> p c t i", i=4),
+                    in0=bank[:].rearrange("p (t c i) -> p c t i", t=4, i=4),
+                    in1=du[i][:, 4 * h : 4 * h + 4, :].rearrange("p t (c i) -> p c t i", i=4),
+                    op=ALU.add,
+                )
+
+        def add_offset(engine, i, lo, hi):
+            engine.tensor_tensor(out=y_sb[i][:, lo:hi], in0=y_sb[i][:, lo:hi], in1=c_bc[:, lo:hi], op=ALU.add)
+
+        def second_stage(i, pool_cols):
+            codes, scales = h_q[i]
+            y_sb[i] = three.tile([P, N], F32, name="y")
+            for j in range(NG):
+                cols = slice(j * BANK, (j + 1) * BANK)
+                bank = ps_mx.tile([P, BANK], F32, name="mx_bank")
+                for g in range(KG):
+                    nc.tensor.matmul_mx(
+                        out=bank[:],
+                        lhsT=codes[:, g * P : (g + 1) * P].bitcast(FP8X4),
+                        lhsT_scale=scales[:, g * P : (g + 1) * P],
+                        rhs=r_words[:, g, 2 * j * BANK : 2 * (j + 1) * BANK].bitcast(FP4X4),
+                        rhs_scale=r_scales[:, g, cols],
+                        start=(g == 0),
+                        stop=(g == KG - 1),
+                    )
+                nc.vector.scalar_tensor_tensor(
+                    out=y_sb[i][:, cols], in0=bank[:], scalar=w_col[:, i : i + 1], in1=v_bc[:, cols],
+                    op0=ALU.mult, op1=ALU.mult,
+                )
+                if j * BANK < pool_cols:
+                    add_offset(nc.gpsimd, i, j * BANK, min((j + 1) * BANK, pool_cols))
+
+        def round_result(copy, i, glo, ghi):
+            if glo == 0:
+                y_pairs[i] = two.tile([P, N], BF16, name="y_pairs")
+            cols = slice(glo * BANK, ghi * BANK)
+            copy(
+                out=y_pairs[i][:, cols].rearrange("p (g u q e) -> p g u q e", g=ghi - glo, u=2, e=2),
+                in_=y_sb[i][:, cols].rearrange("p (g q u e) -> p g u q e", g=ghi - glo, u=2, e=2),
+            )
+
+        def turn_result(i, h, bank):
+            words = y_pairs[i][:].bitcast(F32)
+            y_grouped[i, h] = four.tile([P, 2, P, 4], BF16, name="y_grouped", align_bytes=64)
+            for q in range(4):
+                nc.tensor.transpose(bank[:, q * P : (q + 1) * P], words[:, (4 * h + q) * P : (4 * h + q + 1) * P], ident[:])
+            interleave_out(y_grouped[i, h][:], bank)
+
+        def turn_result_whole(i):
+            for h in range(NG // 2):
+                bank = ps_two.tile([P, BANK], F32, name="y_bank")
+                turn_result(i, h, bank)
+
+        def quantize_result(i):
+            wlo, whi = group_of(WORD_GROUPS, i)
+            slo, shi = group_of(SCALE_GROUPS, i)
+            if i == wlo:
+                word_tiles[wlo] = two.tile([P, NG, (whi - wlo) * P], U32, name="y_codes", align_bytes=64)
+            if i == slo:
+                scale_tiles[slo] = keep.tile([P, NG, (shi - slo) * P], U8, name="y_scales%d" % slo, align_bytes=64)
+            for g in range(NG):
+                nc.vector.quantize_mx(
+                    out=word_tiles[wlo][:, g, (i - wlo) * P : (i - wlo + 1) * P].bitcast(FP8X4),
+                    scales=scale_tiles[slo][:, g, (i - slo) * P : (i - slo + 1) * P],
+                    in_=y_grouped[i, g // 2][:, g % 2, :, :].rearrange("p m t -> p (m t)"),
+                )
+            if i == whi - 1:
+                nc.sync.dma_start(
+                    out=out_1[:, :, wlo * P : whi * P, :].rearrange("g p m t -> p g (m t)").bitcast(I32),
+                    in_=word_tiles[wlo][:].bitcast(I32),
+                )
+            if i == shi - 1:
+                for q in range(4):
+                    queue = nc.scalar if i == TILES - 1 and q % 2 else nc.sync
+                    queue.dma_start(
+                        out=out_2[:, 4 * q : 4 * q + 4, slo * P : shi * P].rearrange("g r m -> r g m").bitcast(I32),
+                        in_=scale_tiles[slo][32 * q : 32 * q + 4, :, :].bitcast(I32),
+                    )
+
+        def live(i):
+            return 0 <= i < TILES
+
+        def store_result(i, lo, hi):
+            nc.sync.dma_start(out=out_0[i * P : (i + 1) * P, lo:hi], in_=y_sb[i][:, lo:hi])
+
+        sort_propagator(0)
+        turn_inputs(0)
+        x_q[0] = quantize(x_grouped[0], "x")
+        sort_propagator(1)
+        spread_w()
+        turn_inputs(1)
+        first_stage(0)
+        x_q[1] = quantize(x_grouped[1], "x")
+        h_q[0] = quantize(h_grouped[0], "h")
+        last = TILES - 1
+        for s in range(last):
+            second_stage(s, POOL_COLS)
+            first_stage(s + 1)
+            add_offset(nc.vector, s, POOL_COLS, N)
+            store_result(s, 0, N)
+            h_q[s + 1] = quantize(h_grouped[s + 1], "h")
+            if live(s + 2):
+                turn_inputs(s + 2)
+            if live(s - 1):
+                turn_result_whole(s - 1)
+            round_result(nc.scalar.copy, s, 0, NG)
+            if live(s - 2):
+                quantize_result(s - 2)
+            if live(s + 2):
+                x_q[s + 2] = quantize(x_grouped[s + 2], "x")
+
+        second_stage(last, LAST_POOL_COLS)
+        add_offset(nc.vector, last, LAST_POOL_COLS, 2 * BANK)
+        store_result(last, 0, 2 * BANK)
+        round_result(nc.scalar.copy, last, 0, 1)
+        round_result(nc.scalar.copy, last, 1, 2)
+        turn_result_whole(last - 1)
+        add_offset(nc.vector, last, 2 * BANK, 3 * BANK)
+        add_offset(nc.vector, last, 3 * BANK, N)
+        store_result(last, 2 * BANK, N)
+        round_result(nc.vector.tensor_copy, last, 2, 3)
+        round_result(nc.vector.tensor_copy, last, 3, 4)
+        x_bank = ps_one.tile([P, BANK], F32, name="x_bank")
+        turn_result(last, 0, x_bank)
+        d_bank = ps_one.tile([P, BANK], F32, name="d_bank")
+        turn_result(last, 1, d_bank)
+        for i in range(last - 2, TILES):
+            quantize_result(i)

@@ -21,11 +21,12 @@ TILES = M // P
 KG = S // 512
 NG = N // 512
 BANK = 512
-POOL_COLS = 1408
-LAST_POOL_COLS = 768
-LOAD_GROUPS = [(0, 1), (1, 2), (2, 3), (3, 6), (6, 9), (9, 12)]
-WORD_GROUPS = [(0, 2), (2, 4), (4, 6), (6, 8), (8, 10), (10, 11), (11, 12)]
-SCALE_GROUPS = [(0, 10), (10, 12)]
+POOL_COLS = 1152
+V_ROW, C_ROW, W_ROW = 0, 8, 32
+VEC_ROWS = W_ROW + TILES
+LOAD_GROUPS = [(0, 1), (1, 2), (2, 3), (3, 4), (4, 6), (6, 9), (9, 12)]
+WORD_GROUPS = [(0, 2), (2, 4), (4, 6), (6, 8), (8, 9), (9, 10), (10, 11), (11, 12)]
+SCALE_GROUPS = [(0, 8), (8, 12)]
 
 
 def group_of(groups, i):
@@ -47,10 +48,10 @@ def tile_pharmacokinetic_tissue_step_h1_kernel(
         ps_mx = ctx.enter_context(tc.psum_pool(name="ps_mx", bufs=4))
         ctx.enter_context(tc.manual_schedule())
 
-        ident = keep.tile([P, P], F32, name="ident")
-        make_identity(nc, ident[:])
         w_square = keep.tile([P, P], F32, name="w_square")
         nc.gpsimd.memset(w_square[:], 0.0)
+        ident = keep.tile([P, P], F32, name="ident")
+        make_identity(nc, ident[:])
 
         p_words = {}
         p_scales = keep.tile([P, KG, S], U8, name="p_scales", align_bytes=64)
@@ -75,7 +76,7 @@ def tile_pharmacokinetic_tissue_step_h1_kernel(
                 )
 
         u_raw = keep.tile([P, KG, 4], BF16, name="u_raw")
-        w_rows = keep.tile([TILES, P], BF16, name="w_rows")
+        w_rows = keep.tile([VEC_ROWS, P], BF16, name="w_rows")
         v_bc = keep.tile([P, N], BF16, name="v_bc")
         c_bc = keep.tile([P, N], BF16, name="c_bc")
 
@@ -87,46 +88,53 @@ def tile_pharmacokinetic_tissue_step_h1_kernel(
             )
 
         load_propagator(0)
+        nc.sync.dma_start(out=w_square[V_ROW : V_ROW + 8, :].bitcast(BF16), in_=inv_volume.rearrange("(i p) -> i p", p=2 * P))
+        nc.sync.dma_start(out=w_square[C_ROW : C_ROW + 8, :].bitcast(BF16), in_=offset.rearrange("(i p) -> i p", p=2 * P))
+        nc.sync.dma_start(out=w_rows[W_ROW:VEC_ROWS, :], in_=inv_size.rearrange("(i p) -> i p", p=P))
         load_rows(x_sb, states, "x", *LOAD_GROUPS[0])
         load_scale_rows(p_scales, propagator_scales)
-        load_propagator(1)
         load_rows(d_sb, doses, "d", *LOAD_GROUPS[0])
+        load_propagator(1)
         nc.sync.dma_start(out=u_raw[:], in_=uptake.rearrange("(g p t) -> p g t", g=KG, t=4))
-        nc.sync.dma_start(out=w_rows[:], in_=inv_size.rearrange("(i p) -> i p", p=P))
         load_rows(x_sb, states, "x", *LOAD_GROUPS[1])
         load_rows(d_sb, doses, "d", *LOAD_GROUPS[1])
         nc.sync.dma_start(out=r_words[:].bitcast(I32), in_=partition_words.rearrange("g p n -> p g n").bitcast(I32))
         load_scale_rows(r_scales, partition_scales)
-        nc.sync.dma_start(out=v_bc[:], in_=inv_volume.partition_broadcast(P))
-        nc.sync.dma_start(out=c_bc[:], in_=offset.partition_broadcast(P))
         for grp in LOAD_GROUPS[2:]:
             load_rows(x_sb, states, "x", *grp)
             load_rows(d_sb, doses, "d", *grp)
 
         u_col = keep.tile([P, KG * 4], F32, name="u_col")
-        nc.scalar.activation(out=u_col[:], in_=u_raw[:].rearrange("p g t -> p (g t)"), func=ACT.Copy)
-        w_col = keep.tile([P, TILES], F32, name="w_col")
+        vec_cols = keep.tile([P, VEC_ROWS], F32, name="vec_cols")
 
         p_words_sorted, p_scales_sorted = {}, {}
 
-        def sort_propagator(h):
-            words = keep.tile([P, KG, 1024], U8, name="p_words_sorted%d" % h, align_bytes=64)
-            scales = keep.tile([P, KG, 512], U8, name="p_scales_sorted%d" % h, align_bytes=64)
+        def sort_words(h):
+            p_words_sorted[h] = keep.tile([P, KG, 1024], U8, name="p_words_sorted%d" % h, align_bytes=64)
             nc.vector.tensor_copy(
-                out=words[:].rearrange("p g (t m b) -> p g t m b", t=4, b=2),
+                out=p_words_sorted[h][:].rearrange("p g (t m b) -> p g t m b", t=4, b=2),
                 in_=p_words[h][:].rearrange("p g (m t b) -> p g t m b", t=4, b=2),
             )
+
+        def sort_scales(h):
+            p_scales_sorted[h] = keep.tile([P, KG, 512], U8, name="p_scales_sorted%d" % h, align_bytes=64)
             nc.vector.tensor_copy(
-                out=scales[:].rearrange("p g (t m) -> p g t m", t=4),
+                out=p_scales_sorted[h][:].rearrange("p g (t m) -> p g t m", t=4),
                 in_=p_scales[:, :, 512 * h : 512 * (h + 1)].rearrange("p g (m t) -> p g t m", t=4),
             )
-            p_words_sorted[h], p_scales_sorted[h] = words, scales
 
-        def spread_w():
-            nc.scalar.activation(out=w_square[0:TILES, :], in_=w_rows[:], func=ACT.Copy)
+        def turn_vectors():
+            nc.scalar.activation(out=w_square[W_ROW:VEC_ROWS, :], in_=w_rows[W_ROW:VEC_ROWS, :], func=ACT.Copy)
             bank = ps_two.tile([P, BANK], F32, name="y_bank")
             nc.tensor.transpose(bank[:, 0:P], w_square[:], ident[:])
-            nc.scalar.copy(out=w_col[:], in_=bank[:, 0:TILES])
+            nc.scalar.copy(out=vec_cols[:], in_=bank[:, 0:VEC_ROWS])
+
+        def spread(dst, row, j, pool, tag):
+            bank = pool.tile([P, BANK], F32, name=tag)
+            for q in range(4):
+                col = row + 4 * j + q
+                nc.tensor.transpose(bank[:, q * P : (q + 1) * P], vec_cols[:, col : col + 1].to_broadcast([P, P]), ident[:])
+            nc.scalar.copy(out=dst[:].bitcast(F32)[:, j * BANK : (j + 1) * BANK], in_=bank[:])
 
         x_grouped, x_q, du, h_grouped, h_q, y_sb, y_pairs, y_grouped = {}, {}, {}, {}, {}, {}, {}, {}
         word_tiles, scale_tiles = {}, {}
@@ -144,11 +152,13 @@ def tile_pharmacokinetic_tissue_step_h1_kernel(
                 in_=bank[:].rearrange("p (g u m) -> p g m u", g=2, u=2),
             )
 
-        def turn_inputs(i):
+        def turn_states(i):
             x_bank = ps_one.tile([P, BANK], F32, name="x_bank")
             turn_pairs(x_bank, x_sb[i])
             x_grouped[i] = two.tile([P, KG, P, 4], BF16, name="x_grouped", align_bytes=64)
             interleave_out(x_grouped[i][:], x_bank)
+
+        def turn_doses(i):
             d_bank = ps_one.tile([P, BANK], F32, name="d_bank")
             turn_pairs(d_bank, d_sb[i])
             du[i] = three.tile([P, KG * 4, P], F32, name="du")
@@ -169,10 +179,11 @@ def tile_pharmacokinetic_tissue_step_h1_kernel(
             nc.vector.quantize_mx(out=codes[:].bitcast(FP8X4), scales=scales[:], in_=src[:].rearrange("p g m t -> p (g m t)"))
             return codes, scales
 
-        def first_stage(i):
+        def first_stage(i, halves=(0, 1)):
             codes, scales = x_q[i]
-            h_grouped[i] = two.tile([P, KG, P, 4], BF16, name="h_grouped", align_bytes=64)
-            for h in range(KG):
+            if halves[0] == 0:
+                h_grouped[i] = two.tile([P, KG, P, 4], BF16, name="h_grouped", align_bytes=64)
+            for h in halves:
                 bank = ps_mx.tile([P, BANK], F32, name="mx_bank")
                 for t in range(4):
                     for g in range(KG):
@@ -186,19 +197,20 @@ def tile_pharmacokinetic_tissue_step_h1_kernel(
                             stop=(g == KG - 1),
                         )
                 nc.vector.tensor_tensor(
-                    out=h_grouped[i][:, h, :, :].rearrange("p (c i) t -> p c t i", i=4),
-                    in0=bank[:].rearrange("p (t c i) -> p c t i", t=4, i=4),
-                    in1=du[i][:, 4 * h : 4 * h + 4, :].rearrange("p t (c i) -> p c t i", i=4),
+                    out=h_grouped[i][:, h, :, :].rearrange("p (c i) t -> p c t i", i=2),
+                    in0=du[i][:, 4 * h : 4 * h + 4, :].rearrange("p t (c i) -> p c t i", i=2),
+                    in1=bank[:].rearrange("p (t c i) -> p c t i", t=4, i=2),
                     op=ALU.add,
                 )
 
         def add_offset(engine, i, lo, hi):
             engine.tensor_tensor(out=y_sb[i][:, lo:hi], in0=y_sb[i][:, lo:hi], in1=c_bc[:, lo:hi], op=ALU.add)
 
-        def second_stage(i, pool_cols):
+        def second_stage(i, jlo, jhi, pool_cols):
             codes, scales = h_q[i]
-            y_sb[i] = three.tile([P, N], F32, name="y")
-            for j in range(NG):
+            if jlo == 0:
+                y_sb[i] = three.tile([P, N], F32, name="y")
+            for j in range(jlo, jhi):
                 cols = slice(j * BANK, (j + 1) * BANK)
                 bank = ps_mx.tile([P, BANK], F32, name="mx_bank")
                 for g in range(KG):
@@ -212,7 +224,7 @@ def tile_pharmacokinetic_tissue_step_h1_kernel(
                         stop=(g == KG - 1),
                     )
                 nc.vector.scalar_tensor_tensor(
-                    out=y_sb[i][:, cols], in0=bank[:], scalar=w_col[:, i : i + 1], in1=v_bc[:, cols],
+                    out=y_sb[i][:, cols], in0=v_bc[:, cols], scalar=vec_cols[:, W_ROW + i : W_ROW + i + 1], in1=bank[:],
                     op0=ALU.mult, op1=ALU.mult,
                 )
                 if j * BANK < pool_cols:
@@ -239,25 +251,25 @@ def tile_pharmacokinetic_tissue_step_h1_kernel(
                 bank = ps_two.tile([P, BANK], F32, name="y_bank")
                 turn_result(i, h, bank)
 
-        def quantize_result(i):
+        def quantize_result(i, glo, ghi):
             wlo, whi = group_of(WORD_GROUPS, i)
             slo, shi = group_of(SCALE_GROUPS, i)
-            if i == wlo:
-                word_tiles[wlo] = two.tile([P, NG, (whi - wlo) * P], U32, name="y_codes", align_bytes=64)
-            if i == slo:
+            if i == wlo and glo == 0:
+                word_tiles[wlo] = three.tile([P, NG, (whi - wlo) * P], U32, name="y_codes", align_bytes=64)
+            if i == slo and glo == 0:
                 scale_tiles[slo] = keep.tile([P, NG, (shi - slo) * P], U8, name="y_scales%d" % slo, align_bytes=64)
-            for g in range(NG):
+            for g in range(glo, ghi):
                 nc.vector.quantize_mx(
                     out=word_tiles[wlo][:, g, (i - wlo) * P : (i - wlo + 1) * P].bitcast(FP8X4),
                     scales=scale_tiles[slo][:, g, (i - slo) * P : (i - slo + 1) * P],
                     in_=y_grouped[i, g // 2][:, g % 2, :, :].rearrange("p m t -> p (m t)"),
                 )
-            if i == whi - 1:
+            if i == whi - 1 and ghi == NG:
                 nc.sync.dma_start(
                     out=out_1[:, :, wlo * P : whi * P, :].rearrange("g p m t -> p g (m t)").bitcast(I32),
                     in_=word_tiles[wlo][:].bitcast(I32),
                 )
-            if i == shi - 1:
+            if i == shi - 1 and ghi == NG:
                 for q in range(4):
                     queue = nc.scalar if i == TILES - 1 and q % 2 else nc.sync
                     queue.dma_start(
@@ -271,46 +283,78 @@ def tile_pharmacokinetic_tissue_step_h1_kernel(
         def store_result(i, lo, hi):
             nc.sync.dma_start(out=out_0[i * P : (i + 1) * P, lo:hi], in_=y_sb[i][:, lo:hi])
 
-        sort_propagator(0)
-        turn_inputs(0)
+        turn_vectors()
+        sort_words(0)
+        sort_scales(0)
+        turn_states(0)
+        nc.scalar.activation(out=u_col[:], in_=u_raw[:].rearrange("p g t -> p (g t)"), func=ACT.Copy)
         x_q[0] = quantize(x_grouped[0], "x")
-        sort_propagator(1)
-        spread_w()
-        turn_inputs(1)
-        first_stage(0)
+        spread(v_bc, V_ROW, 0, ps_two, "y_bank")
+        spread(c_bc, C_ROW, 0, ps_two, "y_bank")
+        turn_doses(0)
+        sort_words(1)
+        sort_scales(1)
+        turn_states(1)
+        first_stage(0, (0,))
         x_q[1] = quantize(x_grouped[1], "x")
+        first_stage(0, (1,))
+        turn_doses(1)
+        spread(v_bc, V_ROW, 1, ps_two, "y_bank")
+        spread(c_bc, C_ROW, 1, ps_two, "y_bank")
         h_q[0] = quantize(h_grouped[0], "h")
+        first_stage(1)
+        turn_states(2)
+        turn_doses(2)
+        x_q[2] = quantize(x_grouped[2], "x")
+        h_q[1] = quantize(h_grouped[1], "h")
         last = TILES - 1
-        for s in range(last):
-            second_stage(s, POOL_COLS)
-            first_stage(s + 1)
+        for s in range(last - 1):
+            second_stage(s, 0, 2, POOL_COLS)
+            if live(s - 2):
+                turn_result_whole(s - 2)
+            if live(s - 1):
+                round_result(nc.scalar.copy, s - 1, 0, NG)
+            second_stage(s, 2, NG, POOL_COLS)
+            first_stage(s + 2)
+            if live(s + 3):
+                turn_states(s + 3)
+                turn_doses(s + 3)
+            else:
+                turn_result_whole(s - 1)
+            if live(s - 2):
+                quantize_result(s - 2, 0, 2)
+            h_q[s + 2] = quantize(h_grouped[s + 2], "h")
             add_offset(nc.vector, s, POOL_COLS, N)
             store_result(s, 0, N)
-            h_q[s + 1] = quantize(h_grouped[s + 1], "h")
-            if live(s + 2):
-                turn_inputs(s + 2)
-            if live(s - 1):
-                turn_result_whole(s - 1)
-            round_result(nc.scalar.copy, s, 0, NG)
             if live(s - 2):
-                quantize_result(s - 2)
-            if live(s + 2):
-                x_q[s + 2] = quantize(x_grouped[s + 2], "x")
+                quantize_result(s - 2, 2, NG)
+            if live(s + 3):
+                x_q[s + 3] = quantize(x_grouped[s + 3], "x")
+            else:
+                quantize_result(s - 1, 0, NG)
 
-        second_stage(last, LAST_POOL_COLS)
-        add_offset(nc.vector, last, LAST_POOL_COLS, 2 * BANK)
-        store_result(last, 0, 2 * BANK)
-        round_result(nc.scalar.copy, last, 0, 1)
-        round_result(nc.scalar.copy, last, 1, 2)
-        turn_result_whole(last - 1)
-        add_offset(nc.vector, last, 2 * BANK, 3 * BANK)
-        add_offset(nc.vector, last, 3 * BANK, N)
-        store_result(last, 2 * BANK, N)
-        round_result(nc.vector.tensor_copy, last, 2, 3)
-        round_result(nc.vector.tensor_copy, last, 3, 4)
+        prev = last - 1
+        round_result(nc.scalar.copy, prev - 1, 0, NG)
+        second_stage(prev, 0, NG, 3 * BANK)
+        store_result(prev, 0, 2 * BANK)
+        second_stage(last, 0, 2, 0)
+        turn_result_whole(prev - 1)
+        second_stage(last, 2, NG, 0)
+        add_offset(nc.vector, prev, 3 * BANK, N)
+        store_result(prev, 2 * BANK, N)
+        for g in range(NG):
+            round_result(nc.scalar.copy, prev, g, g + 1)
+        turn_result_whole(prev)
+        for g in range(NG):
+            add_offset(nc.vector, last, g * BANK, (g + 1) * BANK)
+            if g % 2:
+                store_result(last, (g - 1) * BANK, (g + 1) * BANK)
+        quantize_result(prev - 1, 0, NG)
+        for g in range(NG):
+            round_result(nc.scalar.copy if g < 2 else nc.vector.tensor_copy, last, g, g + 1)
         x_bank = ps_one.tile([P, BANK], F32, name="x_bank")
         turn_result(last, 0, x_bank)
         d_bank = ps_one.tile([P, BANK], F32, name="d_bank")
         turn_result(last, 1, d_bank)
-        for i in range(last - 2, TILES):
-            quantize_result(i)
+        for i in range(prev, TILES):
+            quantize_result(i, 0, NG)

@@ -21,7 +21,8 @@ TILES = M // P
 KG = S // 512
 NG = N // 512
 BANK = 512
-POOL_COLS = 1152
+POOL_COLS = 1344
+POOL_RUNS = [(0, BANK), (BANK, POOL_COLS)]
 V_ROW, C_ROW, W_ROW = 0, 8, 32
 VEC_ROWS = W_ROW + TILES
 LOAD_GROUPS = [(0, 1), (1, 2), (2, 3), (3, 4), (4, 6), (6, 9), (9, 12)]
@@ -44,7 +45,7 @@ def tile_pharmacokinetic_tissue_step_h1_kernel(
         three = ctx.enter_context(tc.tile_pool(name="three", bufs=3))
         four = ctx.enter_context(tc.tile_pool(name="four", bufs=6))
         ps_one = ctx.enter_context(tc.psum_pool(name="ps_one", bufs=1))
-        ps_two = ctx.enter_context(tc.psum_pool(name="ps_two", bufs=2))
+        ps_turn = ctx.enter_context(tc.psum_pool(name="ps_turn", bufs=3))
         ps_mx = ctx.enter_context(tc.psum_pool(name="ps_mx", bufs=4))
         ctx.enter_context(tc.manual_schedule())
 
@@ -88,14 +89,14 @@ def tile_pharmacokinetic_tissue_step_h1_kernel(
             )
 
         load_propagator(0)
-        nc.sync.dma_start(out=w_square[V_ROW : V_ROW + 8, :].bitcast(BF16), in_=inv_volume.rearrange("(i p) -> i p", p=2 * P))
-        nc.sync.dma_start(out=w_square[C_ROW : C_ROW + 8, :].bitcast(BF16), in_=offset.rearrange("(i p) -> i p", p=2 * P))
-        nc.sync.dma_start(out=w_rows[W_ROW:VEC_ROWS, :], in_=inv_size.rearrange("(i p) -> i p", p=P))
         load_rows(x_sb, states, "x", *LOAD_GROUPS[0])
         load_scale_rows(p_scales, propagator_scales)
         load_rows(d_sb, doses, "d", *LOAD_GROUPS[0])
         load_propagator(1)
         nc.sync.dma_start(out=u_raw[:], in_=uptake.rearrange("(g p t) -> p g t", g=KG, t=4))
+        nc.sync.dma_start(out=w_square[V_ROW : V_ROW + 8, :].bitcast(BF16), in_=inv_volume.rearrange("(i p) -> i p", p=2 * P))
+        nc.sync.dma_start(out=w_square[C_ROW : C_ROW + 8, :].bitcast(BF16), in_=offset.rearrange("(i p) -> i p", p=2 * P))
+        nc.sync.dma_start(out=w_rows[W_ROW:VEC_ROWS, :], in_=inv_size.rearrange("(i p) -> i p", p=P))
         load_rows(x_sb, states, "x", *LOAD_GROUPS[1])
         load_rows(d_sb, doses, "d", *LOAD_GROUPS[1])
         nc.sync.dma_start(out=r_words[:].bitcast(I32), in_=partition_words.rearrange("g p n -> p g n").bitcast(I32))
@@ -125,12 +126,15 @@ def tile_pharmacokinetic_tissue_step_h1_kernel(
 
         def turn_vectors():
             nc.scalar.activation(out=w_square[W_ROW:VEC_ROWS, :], in_=w_rows[W_ROW:VEC_ROWS, :], func=ACT.Copy)
-            bank = ps_two.tile([P, BANK], F32, name="y_bank")
+            bank = ps_turn.tile([P, BANK], F32, name="turn_bank")
             nc.tensor.transpose(bank[:, 0:P], w_square[:], ident[:])
             nc.scalar.copy(out=vec_cols[:], in_=bank[:, 0:VEC_ROWS])
 
+        kept = {}
+
         def spread(dst, row, j, pool, tag):
             bank = pool.tile([P, BANK], F32, name=tag)
+            kept[tag] = bank
             for q in range(4):
                 col = row + 4 * j + q
                 nc.tensor.transpose(bank[:, q * P : (q + 1) * P], vec_cols[:, col : col + 1].to_broadcast([P, P]), ident[:])
@@ -153,13 +157,13 @@ def tile_pharmacokinetic_tissue_step_h1_kernel(
             )
 
         def turn_states(i):
-            x_bank = ps_one.tile([P, BANK], F32, name="x_bank")
+            x_bank = ps_turn.tile([P, BANK], F32, name="turn_bank")
             turn_pairs(x_bank, x_sb[i])
             x_grouped[i] = two.tile([P, KG, P, 4], BF16, name="x_grouped", align_bytes=64)
             interleave_out(x_grouped[i][:], x_bank)
 
         def turn_doses(i):
-            d_bank = ps_one.tile([P, BANK], F32, name="d_bank")
+            d_bank = ps_turn.tile([P, BANK], F32, name="turn_bank")
             turn_pairs(d_bank, d_sb[i])
             du[i] = three.tile([P, KG * 4, P], F32, name="du")
             halves = d_bank[:].bitcast(BF16)
@@ -206,7 +210,13 @@ def tile_pharmacokinetic_tissue_step_h1_kernel(
         def add_offset(engine, i, lo, hi):
             engine.tensor_tensor(out=y_sb[i][:, lo:hi], in0=y_sb[i][:, lo:hi], in1=c_bc[:, lo:hi], op=ALU.add)
 
-        def second_stage(i, jlo, jhi, pool_cols):
+        def add_offset_psum(i, lo, hi):
+            c_high = kept["c_bank"][:].bitcast(BF16)
+            nc.vector.tensor_tensor(
+                out=y_sb[i][:, lo:hi], in0=y_sb[i][:, lo:hi], in1=c_high[:, lo - N // 2 : hi - N // 2], op=ALU.add
+            )
+
+        def second_stage(i, jlo, jhi, pool_runs):
             codes, scales = h_q[i]
             if jlo == 0:
                 y_sb[i] = three.tile([P, N], F32, name="y")
@@ -227,8 +237,9 @@ def tile_pharmacokinetic_tissue_step_h1_kernel(
                     out=y_sb[i][:, cols], in0=v_bc[:, cols], scalar=vec_cols[:, W_ROW + i : W_ROW + i + 1], in1=bank[:],
                     op0=ALU.mult, op1=ALU.mult,
                 )
-                if j * BANK < pool_cols:
-                    add_offset(nc.gpsimd, i, j * BANK, min((j + 1) * BANK, pool_cols))
+                for lo, hi in pool_runs:
+                    if (hi - 1) // BANK == j:
+                        add_offset(nc.gpsimd, i, lo, hi)
 
         def round_result(copy, i, glo, ghi):
             if glo == 0:
@@ -248,7 +259,7 @@ def tile_pharmacokinetic_tissue_step_h1_kernel(
 
         def turn_result_whole(i):
             for h in range(NG // 2):
-                bank = ps_two.tile([P, BANK], F32, name="y_bank")
+                bank = ps_turn.tile([P, BANK], F32, name="turn_bank")
                 turn_result(i, h, bank)
 
         def quantize_result(i, glo, ghi):
@@ -283,51 +294,49 @@ def tile_pharmacokinetic_tissue_step_h1_kernel(
         def store_result(i, lo, hi):
             nc.sync.dma_start(out=out_0[i * P : (i + 1) * P, lo:hi], in_=y_sb[i][:, lo:hi])
 
-        turn_vectors()
         sort_words(0)
         sort_scales(0)
         turn_states(0)
         nc.scalar.activation(out=u_col[:], in_=u_raw[:].rearrange("p g t -> p (g t)"), func=ACT.Copy)
         x_q[0] = quantize(x_grouped[0], "x")
-        spread(v_bc, V_ROW, 0, ps_two, "y_bank")
-        spread(c_bc, C_ROW, 0, ps_two, "y_bank")
         turn_doses(0)
         sort_words(1)
         sort_scales(1)
         turn_states(1)
         first_stage(0, (0,))
+        turn_vectors()
         x_q[1] = quantize(x_grouped[1], "x")
         first_stage(0, (1,))
         turn_doses(1)
-        spread(v_bc, V_ROW, 1, ps_two, "y_bank")
-        spread(c_bc, C_ROW, 1, ps_two, "y_bank")
+        spread(v_bc, V_ROW, 0, ps_turn, "turn_bank")
+        spread(c_bc, C_ROW, 0, ps_turn, "turn_bank")
         h_q[0] = quantize(h_grouped[0], "h")
         first_stage(1)
         turn_states(2)
         turn_doses(2)
+        spread(v_bc, V_ROW, 1, ps_turn, "turn_bank")
+        spread(c_bc, C_ROW, 1, ps_one, "c_bank")
         x_q[2] = quantize(x_grouped[2], "x")
         h_q[1] = quantize(h_grouped[1], "h")
         last = TILES - 1
         for s in range(last - 1):
-            second_stage(s, 0, 2, POOL_COLS)
+            second_stage(s, 0, 2, POOL_RUNS)
             if live(s - 2):
                 turn_result_whole(s - 2)
             if live(s - 1):
                 round_result(nc.scalar.copy, s - 1, 0, NG)
-            second_stage(s, 2, NG, POOL_COLS)
+            second_stage(s, 2, NG, POOL_RUNS)
             first_stage(s + 2)
+            add_offset_psum(s, POOL_COLS, N)
+            store_result(s, 0, N)
             if live(s + 3):
                 turn_states(s + 3)
                 turn_doses(s + 3)
             else:
                 turn_result_whole(s - 1)
-            if live(s - 2):
-                quantize_result(s - 2, 0, 2)
             h_q[s + 2] = quantize(h_grouped[s + 2], "h")
-            add_offset(nc.vector, s, POOL_COLS, N)
-            store_result(s, 0, N)
             if live(s - 2):
-                quantize_result(s - 2, 2, NG)
+                quantize_result(s - 2, 0, NG)
             if live(s + 3):
                 x_q[s + 3] = quantize(x_grouped[s + 3], "x")
             else:
@@ -335,26 +344,23 @@ def tile_pharmacokinetic_tissue_step_h1_kernel(
 
         prev = last - 1
         round_result(nc.scalar.copy, prev - 1, 0, NG)
-        second_stage(prev, 0, NG, 3 * BANK)
+        second_stage(prev, 0, NG, [(0, BANK), (BANK, 2 * BANK)])
         store_result(prev, 0, 2 * BANK)
-        second_stage(last, 0, 2, 0)
-        turn_result_whole(prev - 1)
-        second_stage(last, 2, NG, 0)
-        add_offset(nc.vector, prev, 3 * BANK, N)
+        second_stage(last, 0, 2, [(0, BANK), (BANK, 2 * BANK)])
+        add_offset_psum(prev, 2 * BANK, N)
         store_result(prev, 2 * BANK, N)
-        for g in range(NG):
-            round_result(nc.scalar.copy, prev, g, g + 1)
+        turn_result_whole(prev - 1)
+        for g in range(0, NG, 2):
+            round_result(nc.scalar.copy, prev, g, g + 2)
+        second_stage(last, 2, NG, [])
         turn_result_whole(prev)
-        for g in range(NG):
-            add_offset(nc.vector, last, g * BANK, (g + 1) * BANK)
-            if g % 2:
-                store_result(last, (g - 1) * BANK, (g + 1) * BANK)
+        add_offset_psum(last, 2 * BANK, 3 * BANK)
+        add_offset_psum(last, 3 * BANK, N)
+        store_result(last, 0, 2 * BANK)
+        store_result(last, 2 * BANK, N)
+        round_result(nc.scalar.copy, last, 0, 2)
         quantize_result(prev - 1, 0, NG)
-        for g in range(NG):
-            round_result(nc.scalar.copy if g < 2 else nc.vector.tensor_copy, last, g, g + 1)
-        x_bank = ps_one.tile([P, BANK], F32, name="x_bank")
-        turn_result(last, 0, x_bank)
-        d_bank = ps_one.tile([P, BANK], F32, name="d_bank")
-        turn_result(last, 1, d_bank)
+        round_result(nc.vector.tensor_copy, last, 2, NG)
+        turn_result_whole(last)
         for i in range(prev, TILES):
             quantize_result(i, 0, NG)

@@ -17,21 +17,33 @@ ALU = mybir.AluOpType
 ACT = mybir.ActivationFunctionType
 
 P = 128
-TILES = M // P
-KG = S // 512
-NG = N // 512
+PLACES = 4
+GROUP = P * PLACES
 BANK = 512
-POOL_COLS = 1344
-POOL_RUNS = [(0, BANK), (BANK, POOL_COLS)]
-V_ROW, C_ROW, W_ROW = 0, 8, 32
-VEC_ROWS = W_ROW + TILES
-LOAD_GROUPS = [(0, 1), (1, 2), (2, 3), (3, 4), (4, 6), (6, 9), (9, 12)]
-WORD_GROUPS = [(0, 2), (2, 4), (4, 6), (6, 8), (8, 9), (9, 10), (10, 11), (11, 12)]
-SCALE_GROUPS = [(0, 8), (8, 12)]
+TILES = M // P
+S_GROUPS = S // GROUP
+N_GROUPS = N // GROUP
+HALF = N // 2
+
+GPSIMD_COLS = 1408
+GPSIMD_RUNS = [(0, BANK), (BANK, GPSIMD_COLS)]
+GPSIMD_RUNS_AT_END = [(0, BANK), (BANK, HALF)]
+
+LOAD_RANGES = [(0, 1), (1, 2), (2, 3), (3, 4), (4, 6), (6, 9), (9, 12)]
+CODE_RANGES = [(0, 2), (2, 4), (4, 6), (6, 8), (8, 9), (9, 10), (10, 11), (11, 12)]
+SCALE_RANGES = [(0, 8), (8, 12)]
+
+PAIR_ROWS = N // (2 * P)
+V_ROW, C_ROW, W_ROW = 0, PAIR_ROWS, 32
+VECTOR_ROWS = W_ROW + TILES
 
 
-def group_of(groups, i):
-    return [grp for grp in groups if grp[0] <= i < grp[1]][0]
+def range_of(ranges, i):
+    return [r for r in ranges if r[0] <= i < r[1]][0]
+
+
+def live(i):
+    return 0 <= i < TILES
 
 
 def tile_pharmacokinetic_tissue_step_h1_kernel(
@@ -41,114 +53,112 @@ def tile_pharmacokinetic_tissue_step_h1_kernel(
     nc = tc.nc
     with ExitStack() as ctx:
         keep = ctx.enter_context(tc.tile_pool(name="keep", bufs=1))
-        two = ctx.enter_context(tc.tile_pool(name="two", bufs=2))
-        three = ctx.enter_context(tc.tile_pool(name="three", bufs=3))
-        four = ctx.enter_context(tc.tile_pool(name="four", bufs=6))
-        ps_one = ctx.enter_context(tc.psum_pool(name="ps_one", bufs=1))
+        short = ctx.enter_context(tc.tile_pool(name="short", bufs=2))
+        longer = ctx.enter_context(tc.tile_pool(name="longer", bufs=3))
+        turned = ctx.enter_context(tc.tile_pool(name="turned", bufs=6))
+        ps_keep = ctx.enter_context(tc.psum_pool(name="ps_keep", bufs=1))
         ps_turn = ctx.enter_context(tc.psum_pool(name="ps_turn", bufs=3))
         ps_mx = ctx.enter_context(tc.psum_pool(name="ps_mx", bufs=4))
         ctx.enter_context(tc.manual_schedule())
 
-        w_square = keep.tile([P, P], F32, name="w_square")
-        nc.gpsimd.memset(w_square[:], 0.0)
+        square = keep.tile([P, P], F32, name="square")
+        nc.gpsimd.memset(square[:], 0.0)
         ident = keep.tile([P, P], F32, name="ident")
         make_identity(nc, ident[:])
 
-        p_words = {}
-        p_scales = keep.tile([P, KG, S], U8, name="p_scales", align_bytes=64)
-        r_words = keep.tile([P, KG, 2 * N], U8, name="r_words", align_bytes=64)
-        r_scales = keep.tile([P, KG, N], U8, name="r_scales", align_bytes=64)
+        p_scales = keep.tile([P, S_GROUPS, S], U8, name="p_scales", align_bytes=64)
+        r_words = keep.tile([P, S_GROUPS, 2 * N], U8, name="r_words", align_bytes=64)
+        r_scales = keep.tile([P, S_GROUPS, N], U8, name="r_scales", align_bytes=64)
         nc.vector.memset(p_scales[:].bitcast(I32), 0)
         nc.vector.memset(r_scales[:].bitcast(I32), 0)
 
-        x_sb, d_sb = {}, {}
+        u_raw = keep.tile([P, S_GROUPS, PLACES], BF16, name="u_raw")
+        w_rows = keep.tile([VECTOR_ROWS, P], BF16, name="w_rows")
+        u_cols = keep.tile([P, S_GROUPS * PLACES], F32, name="u_cols")
+        vector_cols = keep.tile([P, VECTOR_ROWS], F32, name="vector_cols")
+        v_spread = keep.tile([P, N], BF16, name="v_spread")
+        c_spread = keep.tile([P, N], BF16, name="c_spread")
+        c_bank = ps_keep.tile([P, BANK], F32, name="c_bank")
 
-        def load_rows(store, src, label, lo, hi):
+        x_rows, d_rows, p_words, p_words_sorted, p_scales_sorted = {}, {}, {}, {}, {}
+        x_grouped, x_mx, du, h_grouped, h_mx = {}, {}, {}, {}, {}
+        y, y_pairs, y_grouped, y_codes, y_scales = {}, {}, {}, {}, {}
+
+
+        def load_rows(rows_of, src, label, lo, hi):
             rows = keep.tile([P, hi - lo, S], BF16, name="%s%d" % (label, lo))
             nc.sync.dma_start(out=rows[:], in_=src[lo * P : hi * P, :].rearrange("(i p) k -> p i k", p=P))
             for i in range(lo, hi):
-                store[i] = rows[:, i - lo, :]
+                rows_of[i] = rows[:, i - lo, :]
 
         def load_scale_rows(plane, src):
-            for q in range(4):
+            for quad in range(4):
                 nc.sync.dma_start(
-                    out=plane[32 * q : 32 * q + 4, :, :].bitcast(I32),
-                    in_=src[:, 4 * q : 4 * q + 4, :].rearrange("g r n -> r g n").bitcast(I32),
+                    out=plane[32 * quad : 32 * quad + 4, :, :].bitcast(I32),
+                    in_=src[:, 4 * quad : 4 * quad + 4, :].rearrange("g r n -> r g n").bitcast(I32),
                 )
 
-        u_raw = keep.tile([P, KG, 4], BF16, name="u_raw")
-        w_rows = keep.tile([VEC_ROWS, P], BF16, name="w_rows")
-        v_bc = keep.tile([P, N], BF16, name="v_bc")
-        c_bc = keep.tile([P, N], BF16, name="c_bc")
-
-        def load_propagator(h):
-            p_words[h] = keep.tile([P, KG, 1024], U8, name="p_words%d" % h, align_bytes=64)
+        def load_propagator_words(h):
+            p_words[h] = keep.tile([P, S_GROUPS, 2 * GROUP], U8, name="p_words%d" % h, align_bytes=64)
             nc.sync.dma_start(
                 out=p_words[h][:].bitcast(I32),
-                in_=propagator_words[:, :, 1024 * h : 1024 * (h + 1)].rearrange("g p n -> p g n").bitcast(I32),
+                in_=propagator_words[:, :, 2 * GROUP * h : 2 * GROUP * (h + 1)].rearrange("g p n -> p g n").bitcast(I32),
             )
 
-        load_propagator(0)
-        load_rows(x_sb, states, "x", *LOAD_GROUPS[0])
+        load_propagator_words(0)
+        load_rows(x_rows, states, "x", *LOAD_RANGES[0])
         load_scale_rows(p_scales, propagator_scales)
-        load_rows(d_sb, doses, "d", *LOAD_GROUPS[0])
-        load_propagator(1)
-        nc.sync.dma_start(out=u_raw[:], in_=uptake.rearrange("(g p t) -> p g t", g=KG, t=4))
-        nc.sync.dma_start(out=w_square[V_ROW : V_ROW + 8, :].bitcast(BF16), in_=inv_volume.rearrange("(i p) -> i p", p=2 * P))
-        nc.sync.dma_start(out=w_square[C_ROW : C_ROW + 8, :].bitcast(BF16), in_=offset.rearrange("(i p) -> i p", p=2 * P))
-        nc.sync.dma_start(out=w_rows[W_ROW:VEC_ROWS, :], in_=inv_size.rearrange("(i p) -> i p", p=P))
-        load_rows(x_sb, states, "x", *LOAD_GROUPS[1])
-        load_rows(d_sb, doses, "d", *LOAD_GROUPS[1])
+        load_rows(d_rows, doses, "d", *LOAD_RANGES[0])
+        load_propagator_words(1)
+        nc.sync.dma_start(out=u_raw[:], in_=uptake.rearrange("(g p t) -> p g t", g=S_GROUPS, t=PLACES))
+        for row, vector in ((V_ROW, inv_volume), (C_ROW, offset)):
+            nc.sync.dma_start(
+                out=square[row : row + PAIR_ROWS, :].bitcast(BF16), in_=vector.rearrange("(i p) -> i p", p=2 * P)
+            )
+        nc.sync.dma_start(out=w_rows[W_ROW:VECTOR_ROWS, :], in_=inv_size.rearrange("(i p) -> i p", p=P))
+        load_rows(x_rows, states, "x", *LOAD_RANGES[1])
+        load_rows(d_rows, doses, "d", *LOAD_RANGES[1])
         nc.sync.dma_start(out=r_words[:].bitcast(I32), in_=partition_words.rearrange("g p n -> p g n").bitcast(I32))
         load_scale_rows(r_scales, partition_scales)
-        for grp in LOAD_GROUPS[2:]:
-            load_rows(x_sb, states, "x", *grp)
-            load_rows(d_sb, doses, "d", *grp)
+        for lo, hi in LOAD_RANGES[2:]:
+            load_rows(x_rows, states, "x", lo, hi)
+            load_rows(d_rows, doses, "d", lo, hi)
 
-        u_col = keep.tile([P, KG * 4], F32, name="u_col")
-        vec_cols = keep.tile([P, VEC_ROWS], F32, name="vec_cols")
 
-        p_words_sorted, p_scales_sorted = {}, {}
-
-        def sort_words(h):
-            p_words_sorted[h] = keep.tile([P, KG, 1024], U8, name="p_words_sorted%d" % h, align_bytes=64)
+        def sort_propagator(h):
+            words = keep.tile([P, S_GROUPS, 2 * GROUP], U8, name="p_words_sorted%d" % h, align_bytes=64)
             nc.vector.tensor_copy(
-                out=p_words_sorted[h][:].rearrange("p g (t m b) -> p g t m b", t=4, b=2),
-                in_=p_words[h][:].rearrange("p g (m t b) -> p g t m b", t=4, b=2),
+                out=words[:].rearrange("p g (t m b) -> p g t m b", t=PLACES, b=2),
+                in_=p_words[h][:].rearrange("p g (m t b) -> p g t m b", t=PLACES, b=2),
             )
-
-        def sort_scales(h):
-            p_scales_sorted[h] = keep.tile([P, KG, 512], U8, name="p_scales_sorted%d" % h, align_bytes=64)
+            scales = keep.tile([P, S_GROUPS, GROUP], U8, name="p_scales_sorted%d" % h, align_bytes=64)
             nc.vector.tensor_copy(
-                out=p_scales_sorted[h][:].rearrange("p g (t m) -> p g t m", t=4),
-                in_=p_scales[:, :, 512 * h : 512 * (h + 1)].rearrange("p g (m t) -> p g t m", t=4),
+                out=scales[:].rearrange("p g (t m) -> p g t m", t=PLACES),
+                in_=p_scales[:, :, GROUP * h : GROUP * (h + 1)].rearrange("p g (m t) -> p g t m", t=PLACES),
             )
+            p_words_sorted[h], p_scales_sorted[h] = words, scales
+
+        def turn_bank():
+            bank = ps_turn.tile([P, BANK], F32, name="turn_bank")
+            return bank
 
         def turn_vectors():
-            nc.scalar.activation(out=w_square[W_ROW:VEC_ROWS, :], in_=w_rows[W_ROW:VEC_ROWS, :], func=ACT.Copy)
-            bank = ps_turn.tile([P, BANK], F32, name="turn_bank")
-            nc.tensor.transpose(bank[:, 0:P], w_square[:], ident[:])
-            nc.scalar.copy(out=vec_cols[:], in_=bank[:, 0:VEC_ROWS])
+            bank = turn_bank()
+            nc.tensor.transpose(bank[:, 0:P], square[:], ident[:])
+            nc.scalar.copy(out=vector_cols[:], in_=bank[:, 0:VECTOR_ROWS])
 
-        kept = {}
+        def spread(dst, first_row, half, bank):
+            for q in range(BANK // P):
+                col = first_row + half * (BANK // P) + q
+                nc.tensor.transpose(
+                    bank[:, q * P : (q + 1) * P], vector_cols[:, col : col + 1].to_broadcast([P, P]), ident[:]
+                )
+            nc.scalar.copy(out=dst[:].bitcast(F32)[:, half * BANK : (half + 1) * BANK], in_=bank[:])
 
-        def spread(dst, row, j, pool, tag):
-            bank = pool.tile([P, BANK], F32, name=tag)
-            kept[tag] = bank
-            for q in range(4):
-                col = row + 4 * j + q
-                nc.tensor.transpose(bank[:, q * P : (q + 1) * P], vec_cols[:, col : col + 1].to_broadcast([P, P]), ident[:])
-            nc.scalar.copy(out=dst[:].bitcast(F32)[:, j * BANK : (j + 1) * BANK], in_=bank[:])
 
-        x_grouped, x_q, du, h_grouped, h_q, y_sb, y_pairs, y_grouped = {}, {}, {}, {}, {}, {}, {}, {}
-        word_tiles, scale_tiles = {}, {}
-
-        def turn_pairs(bank, rows):
+        def turn_parity(dst, rows, g, u):
             words = rows.bitcast(F32)
-            for g in range(KG):
-                for u in range(2):
-                    q = 2 * g + u
-                    nc.tensor.transpose(bank[:, q * P : (q + 1) * P], words[:, 256 * g + u : 256 * (g + 1) : 2], ident[:])
+            nc.tensor.transpose(dst, words[:, 2 * P * g + u : 2 * P * (g + 1) : 2], ident[:])
 
         def interleave_out(dst, bank):
             nc.scalar.copy(
@@ -157,73 +167,85 @@ def tile_pharmacokinetic_tissue_step_h1_kernel(
             )
 
         def turn_states(i):
-            x_bank = ps_turn.tile([P, BANK], F32, name="turn_bank")
-            turn_pairs(x_bank, x_sb[i])
-            x_grouped[i] = two.tile([P, KG, P, 4], BF16, name="x_grouped", align_bytes=64)
-            interleave_out(x_grouped[i][:], x_bank)
+            bank = turn_bank()
+            for g in range(S_GROUPS):
+                for u in range(2):
+                    col = (2 * g + u) * P
+                    turn_parity(bank[:, col : col + P], x_rows[i], g, u)
+            x_grouped[i] = longer.tile([P, S_GROUPS, P, PLACES], BF16, name="x_grouped", align_bytes=64)
+            interleave_out(x_grouped[i][:], bank)
 
-        def turn_doses(i):
-            d_bank = ps_turn.tile([P, BANK], F32, name="turn_bank")
-            turn_pairs(d_bank, d_sb[i])
-            du[i] = three.tile([P, KG * 4, P], F32, name="du")
-            halves = d_bank[:].bitcast(BF16)
-            for g in range(KG):
-                for t in range(4):
-                    q = 2 * g + t // 2
-                    nc.scalar.activation(
-                        out=du[i][:, 4 * g + t, :],
-                        in_=halves[:, 256 * q + t % 2 : 256 * (q + 1) : 2],
-                        func=ACT.Copy,
-                        scale=u_col[:, 4 * g + t : 4 * g + t + 1],
-                    )
+        def turn_doses(lo, count):
+            width = count * P
+            scaled = longer.tile([P, S_GROUPS * PLACES, width], F32, name="du")
+            groups_per_bank = BANK // (2 * width)
+            for first in range(0, S_GROUPS, groups_per_bank):
+                bank = turn_bank()
+                groups = range(first, first + groups_per_bank)
+                for g in groups:
+                    for u in range(2):
+                        for n in range(count):
+                            col = (2 * (g - first) + u) * width + n * P
+                            turn_parity(bank[:, col : col + P], d_rows[lo + n], g, u)
+                values = bank[:].bitcast(BF16)
+                for g in groups:
+                    for t in range(PLACES):
+                        start = 2 * (2 * (g - first) + t // 2) * width
+                        nc.scalar.activation(
+                            out=scaled[:, PLACES * g + t, :],
+                            in_=values[:, start + t % 2 : start + 2 * width : 2],
+                            func=ACT.Copy,
+                            scale=u_cols[:, PLACES * g + t : PLACES * g + t + 1],
+                        )
+            for n in range(count):
+                du[lo + n] = scaled[:, :, n * P : (n + 1) * P]
 
-        def quantize(src, label):
-            codes = three.tile([P, KG * P], U32, name=label + "_codes", align_bytes=64)
-            scales = three.tile([P, KG * P], U8, name=label + "_scales", align_bytes=64)
-            nc.vector.quantize_mx(out=codes[:].bitcast(FP8X4), scales=scales[:], in_=src[:].rearrange("p g m t -> p (g m t)"))
+        def quantize_operand(grouped, label):
+            codes = longer.tile([P, S_GROUPS * P], U32, name=label + "_codes", align_bytes=64)
+            scales = longer.tile([P, S_GROUPS * P], U8, name=label + "_scales", align_bytes=64)
+            nc.vector.quantize_mx(
+                out=codes[:].bitcast(FP8X4), scales=scales[:], in_=grouped[:].rearrange("p g m t -> p (g m t)")
+            )
             return codes, scales
 
-        def first_stage(i, halves=(0, 1)):
-            codes, scales = x_q[i]
-            if halves[0] == 0:
-                h_grouped[i] = two.tile([P, KG, P, 4], BF16, name="h_grouped", align_bytes=64)
-            for h in halves:
+        def quantize_states(i):
+            x_mx[i] = quantize_operand(x_grouped[i], "x")
+
+        def quantize_h(i):
+            h_mx[i] = quantize_operand(h_grouped[i], "h")
+
+        def first_stage(i, hlo, hhi):
+            codes, scales = x_mx[i]
+            if hlo == 0:
+                h_grouped[i] = short.tile([P, S_GROUPS, P, PLACES], BF16, name="h_grouped", align_bytes=64)
+            for h in range(hlo, hhi):
                 bank = ps_mx.tile([P, BANK], F32, name="mx_bank")
-                for t in range(4):
-                    for g in range(KG):
+                for t in range(PLACES):
+                    for g in range(S_GROUPS):
                         nc.tensor.matmul_mx(
                             out=bank[:, t * P : (t + 1) * P],
-                            lhsT=p_words_sorted[h][:, g, 256 * t : 256 * (t + 1)].bitcast(FP4X4),
+                            lhsT=p_words_sorted[h][:, g, 2 * P * t : 2 * P * (t + 1)].bitcast(FP4X4),
                             lhsT_scale=p_scales_sorted[h][:, g, P * t : P * (t + 1)],
                             rhs=codes[:, g * P : (g + 1) * P].bitcast(FP8X4),
                             rhs_scale=scales[:, g * P : (g + 1) * P],
                             start=(g == 0),
-                            stop=(g == KG - 1),
+                            stop=(g == S_GROUPS - 1),
                         )
                 nc.vector.tensor_tensor(
                     out=h_grouped[i][:, h, :, :].rearrange("p (c i) t -> p c t i", i=2),
-                    in0=du[i][:, 4 * h : 4 * h + 4, :].rearrange("p t (c i) -> p c t i", i=2),
-                    in1=bank[:].rearrange("p (t c i) -> p c t i", t=4, i=2),
+                    in0=du[i][:, PLACES * h : PLACES * (h + 1), :].rearrange("p t (c i) -> p c t i", i=2),
+                    in1=bank[:].rearrange("p (t c i) -> p c t i", t=PLACES, i=2),
                     op=ALU.add,
                 )
 
-        def add_offset(engine, i, lo, hi):
-            engine.tensor_tensor(out=y_sb[i][:, lo:hi], in0=y_sb[i][:, lo:hi], in1=c_bc[:, lo:hi], op=ALU.add)
-
-        def add_offset_psum(i, lo, hi):
-            c_high = kept["c_bank"][:].bitcast(BF16)
-            nc.vector.tensor_tensor(
-                out=y_sb[i][:, lo:hi], in0=y_sb[i][:, lo:hi], in1=c_high[:, lo - N // 2 : hi - N // 2], op=ALU.add
-            )
-
-        def second_stage(i, jlo, jhi, pool_runs):
-            codes, scales = h_q[i]
+        def second_stage(i, jlo, jhi, gpsimd_runs):
+            codes, scales = h_mx[i]
             if jlo == 0:
-                y_sb[i] = three.tile([P, N], F32, name="y")
+                y[i] = longer.tile([P, N], F32, name="y")
             for j in range(jlo, jhi):
                 cols = slice(j * BANK, (j + 1) * BANK)
                 bank = ps_mx.tile([P, BANK], F32, name="mx_bank")
-                for g in range(KG):
+                for g in range(S_GROUPS):
                     nc.tensor.matmul_mx(
                         out=bank[:],
                         lhsT=codes[:, g * P : (g + 1) * P].bitcast(FP8X4),
@@ -231,136 +253,152 @@ def tile_pharmacokinetic_tissue_step_h1_kernel(
                         rhs=r_words[:, g, 2 * j * BANK : 2 * (j + 1) * BANK].bitcast(FP4X4),
                         rhs_scale=r_scales[:, g, cols],
                         start=(g == 0),
-                        stop=(g == KG - 1),
+                        stop=(g == S_GROUPS - 1),
                     )
                 nc.vector.scalar_tensor_tensor(
-                    out=y_sb[i][:, cols], in0=v_bc[:, cols], scalar=vec_cols[:, W_ROW + i : W_ROW + i + 1], in1=bank[:],
-                    op0=ALU.mult, op1=ALU.mult,
+                    out=y[i][:, cols],
+                    in0=v_spread[:, cols],
+                    scalar=vector_cols[:, W_ROW + i : W_ROW + i + 1],
+                    in1=bank[:],
+                    op0=ALU.mult,
+                    op1=ALU.mult,
                 )
-                for lo, hi in pool_runs:
+                for lo, hi in gpsimd_runs:
                     if (hi - 1) // BANK == j:
-                        add_offset(nc.gpsimd, i, lo, hi)
+                        nc.gpsimd.tensor_tensor(out=y[i][:, lo:hi], in0=y[i][:, lo:hi], in1=c_spread[:, lo:hi], op=ALU.add)
 
-        def round_result(copy, i, glo, ghi):
-            if glo == 0:
-                y_pairs[i] = two.tile([P, N], BF16, name="y_pairs")
-            cols = slice(glo * BANK, ghi * BANK)
-            copy(
-                out=y_pairs[i][:, cols].rearrange("p (g u q e) -> p g u q e", g=ghi - glo, u=2, e=2),
-                in_=y_sb[i][:, cols].rearrange("p (g q u e) -> p g u q e", g=ghi - glo, u=2, e=2),
+        def add_upper_offset(i, lo, hi):
+            c_upper = c_bank[:].bitcast(BF16)
+            nc.vector.tensor_tensor(
+                out=y[i][:, lo:hi], in0=y[i][:, lo:hi], in1=c_upper[:, lo - HALF : hi - HALF], op=ALU.add
             )
 
-        def turn_result(i, h, bank):
+        def store_result(i, lo, hi):
+            nc.sync.dma_start(out=out_0[i * P : (i + 1) * P, lo:hi], in_=y[i][:, lo:hi])
+
+        def round_result(copy, i, glo, ghi):
+            if i not in y_pairs:
+                y_pairs[i] = short.tile([P, N], BF16, name="y_pairs")
+            cols = slice(glo * GROUP, ghi * GROUP)
+            copy(
+                out=y_pairs[i][:, cols].rearrange("p (g u q e) -> p g u q e", g=ghi - glo, u=2, e=2),
+                in_=y[i][:, cols].rearrange("p (g q u e) -> p g u q e", g=ghi - glo, u=2, e=2),
+            )
+
+        def turn_result_half(i, half):
             words = y_pairs[i][:].bitcast(F32)
-            y_grouped[i, h] = four.tile([P, 2, P, 4], BF16, name="y_grouped", align_bytes=64)
-            for q in range(4):
-                nc.tensor.transpose(bank[:, q * P : (q + 1) * P], words[:, (4 * h + q) * P : (4 * h + q + 1) * P], ident[:])
-            interleave_out(y_grouped[i, h][:], bank)
+            bank = turn_bank()
+            for q in range(BANK // P):
+                col = half * BANK + q * P
+                nc.tensor.transpose(bank[:, q * P : (q + 1) * P], words[:, col : col + P], ident[:])
+            y_grouped[i, half] = turned.tile([P, 2, P, PLACES], BF16, name="y_grouped", align_bytes=64)
+            interleave_out(y_grouped[i, half][:], bank)
 
-        def turn_result_whole(i):
-            for h in range(NG // 2):
-                bank = ps_turn.tile([P, BANK], F32, name="turn_bank")
-                turn_result(i, h, bank)
+        def turn_result(i):
+            for half in range(2):
+                turn_result_half(i, half)
 
-        def quantize_result(i, glo, ghi):
-            wlo, whi = group_of(WORD_GROUPS, i)
-            slo, shi = group_of(SCALE_GROUPS, i)
-            if i == wlo and glo == 0:
-                word_tiles[wlo] = three.tile([P, NG, (whi - wlo) * P], U32, name="y_codes", align_bytes=64)
-            if i == slo and glo == 0:
-                scale_tiles[slo] = keep.tile([P, NG, (shi - slo) * P], U8, name="y_scales%d" % slo, align_bytes=64)
-            for g in range(glo, ghi):
+        def quantize_result(i, groups):
+            clo, chi = range_of(CODE_RANGES, i)
+            slo, shi = range_of(SCALE_RANGES, i)
+            if i == clo:
+                y_codes[clo] = longer.tile([P, N_GROUPS, (chi - clo) * P], U32, name="y_codes", align_bytes=64)
+            if i == slo:
+                y_scales[slo] = keep.tile([P, N_GROUPS, (shi - slo) * P], U8, name="y_scales%d" % slo, align_bytes=64)
+            for g in groups:
                 nc.vector.quantize_mx(
-                    out=word_tiles[wlo][:, g, (i - wlo) * P : (i - wlo + 1) * P].bitcast(FP8X4),
-                    scales=scale_tiles[slo][:, g, (i - slo) * P : (i - slo + 1) * P],
+                    out=y_codes[clo][:, g, (i - clo) * P : (i - clo + 1) * P].bitcast(FP8X4),
+                    scales=y_scales[slo][:, g, (i - slo) * P : (i - slo + 1) * P],
                     in_=y_grouped[i, g // 2][:, g % 2, :, :].rearrange("p m t -> p (m t)"),
                 )
-            if i == whi - 1 and ghi == NG:
+            if i == chi - 1:
                 nc.sync.dma_start(
-                    out=out_1[:, :, wlo * P : whi * P, :].rearrange("g p m t -> p g (m t)").bitcast(I32),
-                    in_=word_tiles[wlo][:].bitcast(I32),
+                    out=out_1[:, :, clo * P : chi * P, :].rearrange("g p m t -> p g (m t)").bitcast(I32),
+                    in_=y_codes[clo][:].bitcast(I32),
                 )
-            if i == shi - 1 and ghi == NG:
-                for q in range(4):
-                    queue = nc.scalar if i == TILES - 1 and q % 2 else nc.sync
+            if i == shi - 1:
+                for quad in range(4):
+                    queue = nc.scalar if i == TILES - 1 and quad % 2 else nc.sync
                     queue.dma_start(
-                        out=out_2[:, 4 * q : 4 * q + 4, slo * P : shi * P].rearrange("g r m -> r g m").bitcast(I32),
-                        in_=scale_tiles[slo][32 * q : 32 * q + 4, :, :].bitcast(I32),
+                        out=out_2[:, 4 * quad : 4 * quad + 4, slo * P : shi * P].rearrange("g r m -> r g m").bitcast(I32),
+                        in_=y_scales[slo][32 * quad : 32 * quad + 4, :, :].bitcast(I32),
                     )
 
-        def live(i):
-            return 0 <= i < TILES
+        all_groups = range(N_GROUPS)
 
-        def store_result(i, lo, hi):
-            nc.sync.dma_start(out=out_0[i * P : (i + 1) * P, lo:hi], in_=y_sb[i][:, lo:hi])
-
-        sort_words(0)
-        sort_scales(0)
+        sort_propagator(0)
         turn_states(0)
-        nc.scalar.activation(out=u_col[:], in_=u_raw[:].rearrange("p g t -> p (g t)"), func=ACT.Copy)
-        x_q[0] = quantize(x_grouped[0], "x")
-        turn_doses(0)
-        sort_words(1)
-        sort_scales(1)
+        nc.scalar.activation(out=u_cols[:], in_=u_raw[:].rearrange("p g t -> p (g t)"), func=ACT.Copy)
+        quantize_states(0)
+        turn_doses(0, 1)
+        sort_propagator(1)
+        nc.scalar.activation(out=square[W_ROW:VECTOR_ROWS, :], in_=w_rows[W_ROW:VECTOR_ROWS, :], func=ACT.Copy)
+        first_stage(0, 0, 1)
         turn_states(1)
-        first_stage(0, (0,))
         turn_vectors()
-        x_q[1] = quantize(x_grouped[1], "x")
-        first_stage(0, (1,))
-        turn_doses(1)
-        spread(v_bc, V_ROW, 0, ps_turn, "turn_bank")
-        spread(c_bc, C_ROW, 0, ps_turn, "turn_bank")
-        h_q[0] = quantize(h_grouped[0], "h")
-        first_stage(1)
+        quantize_states(1)
+        first_stage(0, 1, 2)
+        turn_doses(1, 1)
+        spread(v_spread, V_ROW, 0, turn_bank())
+        spread(c_spread, C_ROW, 0, turn_bank())
+        quantize_h(0)
+        first_stage(1, 0, S_GROUPS)
         turn_states(2)
-        turn_doses(2)
-        spread(v_bc, V_ROW, 1, ps_turn, "turn_bank")
-        spread(c_bc, C_ROW, 1, ps_one, "c_bank")
-        x_q[2] = quantize(x_grouped[2], "x")
-        h_q[1] = quantize(h_grouped[1], "h")
+        spread(v_spread, V_ROW, 1, turn_bank())
+        spread(c_spread, C_ROW, 1, c_bank)
+        turn_doses(2, 1)
+        quantize_states(2)
+        quantize_h(1)
+
         last = TILES - 1
         for s in range(last - 1):
-            second_stage(s, 0, 2, POOL_RUNS)
+            second_stage(s, 0, 2, GPSIMD_RUNS)
             if live(s - 2):
-                turn_result_whole(s - 2)
+                turn_result(s - 2)
             if live(s - 1):
-                round_result(nc.scalar.copy, s - 1, 0, NG)
-            second_stage(s, 2, NG, POOL_RUNS)
-            first_stage(s + 2)
-            add_offset_psum(s, POOL_COLS, N)
+                round_result(nc.scalar.copy, s - 1, 0, N_GROUPS)
+            second_stage(s, 2, N_GROUPS, GPSIMD_RUNS)
+            first_stage(s + 2, 0, S_GROUPS)
+            add_upper_offset(s, GPSIMD_COLS, N)
             store_result(s, 0, N)
-            if live(s + 3):
+            if s == 0:
+                turn_states(3)
+            if not live(s + 3):
+                turn_result(s - 1)
+            elif s % 2 == 0:
+                turn_doses(s + 3, min(2, TILES - s - 3))
+            else:
                 turn_states(s + 3)
-                turn_doses(s + 3)
-            else:
-                turn_result_whole(s - 1)
-            h_q[s + 2] = quantize(h_grouped[s + 2], "h")
+                turn_states(s + 4)
+            quantize_h(s + 2)
             if live(s - 2):
-                quantize_result(s - 2, 0, NG)
+                quantize_result(s - 2, all_groups)
             if live(s + 3):
-                x_q[s + 3] = quantize(x_grouped[s + 3], "x")
+                quantize_states(s + 3)
             else:
-                quantize_result(s - 1, 0, NG)
+                quantize_result(s - 1, all_groups)
 
         prev = last - 1
-        round_result(nc.scalar.copy, prev - 1, 0, NG)
-        second_stage(prev, 0, NG, [(0, BANK), (BANK, 2 * BANK)])
-        store_result(prev, 0, 2 * BANK)
-        second_stage(last, 0, 2, [(0, BANK), (BANK, 2 * BANK)])
-        add_offset_psum(prev, 2 * BANK, N)
-        store_result(prev, 2 * BANK, N)
-        turn_result_whole(prev - 1)
-        for g in range(0, NG, 2):
-            round_result(nc.scalar.copy, prev, g, g + 2)
-        second_stage(last, 2, NG, [])
-        turn_result_whole(prev)
-        add_offset_psum(last, 2 * BANK, 3 * BANK)
-        add_offset_psum(last, 3 * BANK, N)
-        store_result(last, 0, 2 * BANK)
-        store_result(last, 2 * BANK, N)
+        round_result(nc.scalar.copy, prev - 1, 0, N_GROUPS)
+        second_stage(prev, 0, N_GROUPS, GPSIMD_RUNS_AT_END)
+        store_result(prev, 0, HALF)
+        second_stage(last, 0, 2, GPSIMD_RUNS_AT_END)
+        add_upper_offset(prev, HALF, N)
+        store_result(prev, HALF, N)
+        turn_result(prev - 1)
+        round_result(nc.scalar.copy, prev, 0, 2)
+        round_result(nc.scalar.copy, prev, 2, N_GROUPS)
+        second_stage(last, 2, N_GROUPS, GPSIMD_RUNS_AT_END)
+        turn_result(prev)
+        for g in range(2, N_GROUPS):
+            add_upper_offset(last, g * GROUP, (g + 1) * GROUP)
+        store_result(last, 0, HALF)
+        store_result(last, HALF, N)
         round_result(nc.scalar.copy, last, 0, 2)
-        quantize_result(prev - 1, 0, NG)
-        round_result(nc.vector.tensor_copy, last, 2, NG)
-        turn_result_whole(last)
-        for i in range(prev, TILES):
-            quantize_result(i, 0, NG)
+        for g in range(2, N_GROUPS):
+            round_result(nc.vector.tensor_copy, last, g, g + 1)
+        turn_result_half(last, 1)
+        turn_result_half(last, 0)
+        quantize_result(prev - 1, all_groups)
+        quantize_result(prev, all_groups)
+        quantize_result(last, (2, 3, 0, 1))

from contextlib import ExitStack

import concourse.mybir as mybir
from concourse.masks import make_identity

M, S, N = 1536, 1024, 2048
FLOPS = 2 * M * S * S + 2 * M * S * N

F32 = mybir.dt.float32
BF16 = mybir.dt.bfloat16
I32 = mybir.dt.int32
U32 = mybir.dt.uint32
U8 = mybir.dt.uint8
FP8X4 = mybir.dt.float8_e4m3fn_x4
FP4X4 = mybir.dt.float4_e2m1fn_x4
ALU = mybir.AluOpType
ACT = mybir.ActivationFunctionType

P = 128
PLACES = 4
GROUP = P * PLACES
BANK = 512
TILES = M // P
S_GROUPS = S // GROUP
N_GROUPS = N // GROUP
HALF = N // 2

GPSIMD_COLS = 1408
GPSIMD_RUNS = [(0, BANK), (BANK, GPSIMD_COLS)]
GPSIMD_RUNS_AT_END = [(0, BANK), (BANK, HALF)]

LOAD_RANGES = [(0, 1), (1, 2), (2, 3), (3, 4), (4, 6), (6, 9), (9, 12)]
CODE_RANGES = [(0, 2), (2, 4), (4, 6), (6, 8), (8, 9), (9, 10), (10, 11), (11, 12)]
SCALE_RANGES = [(0, 8), (8, 12)]

PAIR_ROWS = N // (2 * P)
V_ROW, C_ROW, W_ROW = 0, PAIR_ROWS, 32
VECTOR_ROWS = W_ROW + TILES


def range_of(ranges, i):
    return [r for r in ranges if r[0] <= i < r[1]][0]


def live(i):
    return 0 <= i < TILES


def tile_pharmacokinetic_tissue_step_h1_kernel(
    tc, states, propagator_words, propagator_scales, doses, uptake, partition_words, partition_scales,
    inv_volume, inv_size, offset, out_0, out_1, out_2,
):
    nc = tc.nc
    with ExitStack() as ctx:
        keep = ctx.enter_context(tc.tile_pool(name="keep", bufs=1))
        short = ctx.enter_context(tc.tile_pool(name="short", bufs=2))
        longer = ctx.enter_context(tc.tile_pool(name="longer", bufs=3))
        turned = ctx.enter_context(tc.tile_pool(name="turned", bufs=6))
        ps_keep = ctx.enter_context(tc.psum_pool(name="ps_keep", bufs=1))
        ps_turn = ctx.enter_context(tc.psum_pool(name="ps_turn", bufs=3))
        ps_mx = ctx.enter_context(tc.psum_pool(name="ps_mx", bufs=4))
        ctx.enter_context(tc.manual_schedule())

        square = keep.tile([P, P], F32, name="square")
        nc.gpsimd.memset(square[:], 0.0)
        ident = keep.tile([P, P], F32, name="ident")
        make_identity(nc, ident[:])

        p_scales = keep.tile([P, S_GROUPS, S], U8, name="p_scales", align_bytes=64)
        r_words = keep.tile([P, S_GROUPS, 2 * N], U8, name="r_words", align_bytes=64)
        r_scales = keep.tile([P, S_GROUPS, N], U8, name="r_scales", align_bytes=64)
        nc.vector.memset(p_scales[:].bitcast(I32), 0)
        nc.vector.memset(r_scales[:].bitcast(I32), 0)

        u_raw = keep.tile([P, S_GROUPS, PLACES], BF16, name="u_raw")
        w_rows = keep.tile([VECTOR_ROWS, P], BF16, name="w_rows")
        u_cols = keep.tile([P, S_GROUPS * PLACES], F32, name="u_cols")
        vector_cols = keep.tile([P, VECTOR_ROWS], F32, name="vector_cols")
        v_spread = keep.tile([P, N], BF16, name="v_spread")
        c_spread = keep.tile([P, N], BF16, name="c_spread")
        c_bank = ps_keep.tile([P, BANK], F32, name="c_bank")

        x_rows, d_rows, p_words, p_words_sorted, p_scales_sorted = {}, {}, {}, {}, {}
        x_grouped, x_mx, du, h_grouped, h_mx = {}, {}, {}, {}, {}
        y, y_pairs, y_grouped, y_codes, y_scales = {}, {}, {}, {}, {}


        def load_rows(rows_of, src, label, lo, hi):
            rows = keep.tile([P, hi - lo, S], BF16, name="%s%d" % (label, lo))
            nc.sync.dma_start(out=rows[:], in_=src[lo * P : hi * P, :].rearrange("(i p) k -> p i k", p=P))
            for i in range(lo, hi):
                rows_of[i] = rows[:, i - lo, :]

        def load_scale_rows(plane, src):
            for quad in range(4):
                nc.sync.dma_start(
                    out=plane[32 * quad : 32 * quad + 4, :, :].bitcast(I32),
                    in_=src[:, 4 * quad : 4 * quad + 4, :].rearrange("g r n -> r g n").bitcast(I32),
                )

        def load_propagator_words(h):
            p_words[h] = keep.tile([P, S_GROUPS, 2 * GROUP], U8, name="p_words%d" % h, align_bytes=64)
            nc.sync.dma_start(
                out=p_words[h][:].bitcast(I32),
                in_=propagator_words[:, :, 2 * GROUP * h : 2 * GROUP * (h + 1)].rearrange("g p n -> p g n").bitcast(I32),
            )

        load_propagator_words(0)
        load_rows(x_rows, states, "x", *LOAD_RANGES[0])
        load_scale_rows(p_scales, propagator_scales)
        load_rows(d_rows, doses, "d", *LOAD_RANGES[0])
        load_propagator_words(1)
        nc.sync.dma_start(out=u_raw[:], in_=uptake.rearrange("(g p t) -> p g t", g=S_GROUPS, t=PLACES))
        for row, vector in ((V_ROW, inv_volume), (C_ROW, offset)):
            nc.sync.dma_start(
                out=square[row : row + PAIR_ROWS, :].bitcast(BF16), in_=vector.rearrange("(i p) -> i p", p=2 * P)
            )
        nc.sync.dma_start(out=w_rows[W_ROW:VECTOR_ROWS, :], in_=inv_size.rearrange("(i p) -> i p", p=P))
        load_rows(x_rows, states, "x", *LOAD_RANGES[1])
        load_rows(d_rows, doses, "d", *LOAD_RANGES[1])
        nc.sync.dma_start(out=r_words[:].bitcast(I32), in_=partition_words.rearrange("g p n -> p g n").bitcast(I32))
        load_scale_rows(r_scales, partition_scales)
        for lo, hi in LOAD_RANGES[2:]:
            load_rows(x_rows, states, "x", lo, hi)
            load_rows(d_rows, doses, "d", lo, hi)


        def sort_propagator(h):
            words = keep.tile([P, S_GROUPS, 2 * GROUP], U8, name="p_words_sorted%d" % h, align_bytes=64)
            nc.vector.tensor_copy(
                out=words[:].rearrange("p g (t m b) -> p g t m b", t=PLACES, b=2),
                in_=p_words[h][:].rearrange("p g (m t b) -> p g t m b", t=PLACES, b=2),
            )
            scales = keep.tile([P, S_GROUPS, GROUP], U8, name="p_scales_sorted%d" % h, align_bytes=64)
            nc.vector.tensor_copy(
                out=scales[:].rearrange("p g (t m) -> p g t m", t=PLACES),
                in_=p_scales[:, :, GROUP * h : GROUP * (h + 1)].rearrange("p g (m t) -> p g t m", t=PLACES),
            )
            p_words_sorted[h], p_scales_sorted[h] = words, scales

        def turn_bank():
            bank = ps_turn.tile([P, BANK], F32, name="turn_bank")
            return bank

        def turn_vectors():
            bank = turn_bank()
            nc.tensor.transpose(bank[:, 0:P], square[:], ident[:])
            nc.scalar.copy(out=vector_cols[:], in_=bank[:, 0:VECTOR_ROWS])

        def spread(dst, first_row, half, bank):
            for q in range(BANK // P):
                col = first_row + half * (BANK // P) + q
                nc.tensor.transpose(
                    bank[:, q * P : (q + 1) * P], vector_cols[:, col : col + 1].to_broadcast([P, P]), ident[:]
                )
            nc.scalar.copy(out=dst[:].bitcast(F32)[:, half * BANK : (half + 1) * BANK], in_=bank[:])


        def turn_parity(dst, rows, g, u):
            words = rows.bitcast(F32)
            nc.tensor.transpose(dst, words[:, 2 * P * g + u : 2 * P * (g + 1) : 2], ident[:])

        def interleave_out(dst, bank):
            nc.scalar.copy(
                out=dst.rearrange("p g m t -> p g (m t)").bitcast(F32).rearrange("p g (m u) -> p g m u", u=2),
                in_=bank[:].rearrange("p (g u m) -> p g m u", g=2, u=2),
            )

        def turn_states(i):
            bank = turn_bank()
            for g in range(S_GROUPS):
                for u in range(2):
                    col = (2 * g + u) * P
                    turn_parity(bank[:, col : col + P], x_rows[i], g, u)
            x_grouped[i] = longer.tile([P, S_GROUPS, P, PLACES], BF16, name="x_grouped", align_bytes=64)
            interleave_out(x_grouped[i][:], bank)

        def turn_doses(lo, count):
            width = count * P
            scaled = longer.tile([P, S_GROUPS * PLACES, width], F32, name="du")
            groups_per_bank = BANK // (2 * width)
            for first in range(0, S_GROUPS, groups_per_bank):
                bank = turn_bank()
                groups = range(first, first + groups_per_bank)
                for g in groups:
                    for u in range(2):
                        for n in range(count):
                            col = (2 * (g - first) + u) * width + n * P
                            turn_parity(bank[:, col : col + P], d_rows[lo + n], g, u)
                values = bank[:].bitcast(BF16)
                for g in groups:
                    for t in range(PLACES):
                        start = 2 * (2 * (g - first) + t // 2) * width
                        nc.scalar.activation(
                            out=scaled[:, PLACES * g + t, :],
                            in_=values[:, start + t % 2 : start + 2 * width : 2],
                            func=ACT.Copy,
                            scale=u_cols[:, PLACES * g + t : PLACES * g + t + 1],
                        )
            for n in range(count):
                du[lo + n] = scaled[:, :, n * P : (n + 1) * P]

        def quantize_operand(grouped, label):
            codes = longer.tile([P, S_GROUPS * P], U32, name=label + "_codes", align_bytes=64)
            scales = longer.tile([P, S_GROUPS * P], U8, name=label + "_scales", align_bytes=64)
            nc.vector.quantize_mx(
                out=codes[:].bitcast(FP8X4), scales=scales[:], in_=grouped[:].rearrange("p g m t -> p (g m t)")
            )
            return codes, scales

        def quantize_states(i):
            x_mx[i] = quantize_operand(x_grouped[i], "x")

        def quantize_h(i):
            h_mx[i] = quantize_operand(h_grouped[i], "h")

        def first_stage(i, hlo, hhi):
            codes, scales = x_mx[i]
            if hlo == 0:
                h_grouped[i] = short.tile([P, S_GROUPS, P, PLACES], BF16, name="h_grouped", align_bytes=64)
            for h in range(hlo, hhi):
                bank = ps_mx.tile([P, BANK], F32, name="mx_bank")
                for t in range(PLACES):
                    for g in range(S_GROUPS):
                        nc.tensor.matmul_mx(
                            out=bank[:, t * P : (t + 1) * P],
                            lhsT=p_words_sorted[h][:, g, 2 * P * t : 2 * P * (t + 1)].bitcast(FP4X4),
                            lhsT_scale=p_scales_sorted[h][:, g, P * t : P * (t + 1)],
                            rhs=codes[:, g * P : (g + 1) * P].bitcast(FP8X4),
                            rhs_scale=scales[:, g * P : (g + 1) * P],
                            start=(g == 0),
                            stop=(g == S_GROUPS - 1),
                        )
                nc.vector.tensor_tensor(
                    out=h_grouped[i][:, h, :, :].rearrange("p (c i) t -> p c t i", i=2),
                    in0=du[i][:, PLACES * h : PLACES * (h + 1), :].rearrange("p t (c i) -> p c t i", i=2),
                    in1=bank[:].rearrange("p (t c i) -> p c t i", t=PLACES, i=2),
                    op=ALU.add,
                )

        def second_stage(i, jlo, jhi, gpsimd_runs):
            codes, scales = h_mx[i]
            if jlo == 0:
                y[i] = longer.tile([P, N], F32, name="y")
            for j in range(jlo, jhi):
                cols = slice(j * BANK, (j + 1) * BANK)
                bank = ps_mx.tile([P, BANK], F32, name="mx_bank")
                for g in range(S_GROUPS):
                    nc.tensor.matmul_mx(
                        out=bank[:],
                        lhsT=codes[:, g * P : (g + 1) * P].bitcast(FP8X4),
                        lhsT_scale=scales[:, g * P : (g + 1) * P],
                        rhs=r_words[:, g, 2 * j * BANK : 2 * (j + 1) * BANK].bitcast(FP4X4),
                        rhs_scale=r_scales[:, g, cols],
                        start=(g == 0),
                        stop=(g == S_GROUPS - 1),
                    )
                nc.vector.scalar_tensor_tensor(
                    out=y[i][:, cols],
                    in0=v_spread[:, cols],
                    scalar=vector_cols[:, W_ROW + i : W_ROW + i + 1],
                    in1=bank[:],
                    op0=ALU.mult,
                    op1=ALU.mult,
                )
                for lo, hi in gpsimd_runs:
                    if (hi - 1) // BANK == j:
                        nc.gpsimd.tensor_tensor(out=y[i][:, lo:hi], in0=y[i][:, lo:hi], in1=c_spread[:, lo:hi], op=ALU.add)

        def add_upper_offset(i, lo, hi):
            c_upper = c_bank[:].bitcast(BF16)
            nc.vector.tensor_tensor(
                out=y[i][:, lo:hi], in0=y[i][:, lo:hi], in1=c_upper[:, lo - HALF : hi - HALF], op=ALU.add
            )

        def store_result(i, lo, hi):
            nc.sync.dma_start(out=out_0[i * P : (i + 1) * P, lo:hi], in_=y[i][:, lo:hi])

        def round_result(copy, i, glo, ghi):
            if i not in y_pairs:
                y_pairs[i] = short.tile([P, N], BF16, name="y_pairs")
            cols = slice(glo * GROUP, ghi * GROUP)
            copy(
                out=y_pairs[i][:, cols].rearrange("p (g u q e) -> p g u q e", g=ghi - glo, u=2, e=2),
                in_=y[i][:, cols].rearrange("p (g q u e) -> p g u q e", g=ghi - glo, u=2, e=2),
            )

        def turn_result_half(i, half):
            words = y_pairs[i][:].bitcast(F32)
            bank = turn_bank()
            for q in range(BANK // P):
                col = half * BANK + q * P
                nc.tensor.transpose(bank[:, q * P : (q + 1) * P], words[:, col : col + P], ident[:])
            y_grouped[i, half] = turned.tile([P, 2, P, PLACES], BF16, name="y_grouped", align_bytes=64)
            interleave_out(y_grouped[i, half][:], bank)

        def turn_result(i):
            for half in range(2):
                turn_result_half(i, half)

        def quantize_result(i, groups):
            clo, chi = range_of(CODE_RANGES, i)
            slo, shi = range_of(SCALE_RANGES, i)
            if i == clo:
                y_codes[clo] = longer.tile([P, N_GROUPS, (chi - clo) * P], U32, name="y_codes", align_bytes=64)
            if i == slo:
                y_scales[slo] = keep.tile([P, N_GROUPS, (shi - slo) * P], U8, name="y_scales%d" % slo, align_bytes=64)
            for g in groups:
                nc.vector.quantize_mx(
                    out=y_codes[clo][:, g, (i - clo) * P : (i - clo + 1) * P].bitcast(FP8X4),
                    scales=y_scales[slo][:, g, (i - slo) * P : (i - slo + 1) * P],
                    in_=y_grouped[i, g // 2][:, g % 2, :, :].rearrange("p m t -> p (m t)"),
                )
            if i == chi - 1:
                nc.sync.dma_start(
                    out=out_1[:, :, clo * P : chi * P, :].rearrange("g p m t -> p g (m t)").bitcast(I32),
                    in_=y_codes[clo][:].bitcast(I32),
                )
            if i == shi - 1:
                for quad in range(4):
                    queue = nc.scalar if i == TILES - 1 and quad % 2 else nc.sync
                    queue.dma_start(
                        out=out_2[:, 4 * quad : 4 * quad + 4, slo * P : shi * P].rearrange("g r m -> r g m").bitcast(I32),
                        in_=y_scales[slo][32 * quad : 32 * quad + 4, :, :].bitcast(I32),
                    )

        all_groups = range(N_GROUPS)

        sort_propagator(0)
        turn_states(0)
        nc.scalar.activation(out=u_cols[:], in_=u_raw[:].rearrange("p g t -> p (g t)"), func=ACT.Copy)
        quantize_states(0)
        turn_doses(0, 1)
        sort_propagator(1)
        nc.scalar.activation(out=square[W_ROW:VECTOR_ROWS, :], in_=w_rows[W_ROW:VECTOR_ROWS, :], func=ACT.Copy)
        first_stage(0, 0, 1)
        turn_states(1)
        turn_vectors()
        quantize_states(1)
        first_stage(0, 1, 2)
        turn_doses(1, 1)
        spread(v_spread, V_ROW, 0, turn_bank())
        spread(c_spread, C_ROW, 0, turn_bank())
        quantize_h(0)
        first_stage(1, 0, S_GROUPS)
        turn_states(2)
        spread(v_spread, V_ROW, 1, turn_bank())
        spread(c_spread, C_ROW, 1, c_bank)
        turn_doses(2, 1)
        quantize_states(2)
        quantize_h(1)

        last = TILES - 1
        for s in range(last - 1):
            second_stage(s, 0, 2, GPSIMD_RUNS)
            if live(s - 2):
                turn_result(s - 2)
            if live(s - 1):
                round_result(nc.scalar.copy, s - 1, 0, N_GROUPS)
            second_stage(s, 2, N_GROUPS, GPSIMD_RUNS)
            first_stage(s + 2, 0, S_GROUPS)
            add_upper_offset(s, GPSIMD_COLS, N)
            store_result(s, 0, N)
            if s == 0:
                turn_states(3)
            if not live(s + 3):
                turn_result(s - 1)
            elif s % 2 == 0:
                turn_doses(s + 3, min(2, TILES - s - 3))
            else:
                turn_states(s + 3)
                turn_states(s + 4)
            quantize_h(s + 2)
            if live(s - 2):
                quantize_result(s - 2, all_groups)
            if live(s + 3):
                quantize_states(s + 3)
            else:
                quantize_result(s - 1, all_groups)

        prev = last - 1
        round_result(nc.scalar.copy, prev - 1, 0, N_GROUPS)
        second_stage(prev, 0, N_GROUPS, GPSIMD_RUNS_AT_END)
        store_result(prev, 0, HALF)
        second_stage(last, 0, 2, GPSIMD_RUNS_AT_END)
        add_upper_offset(prev, HALF, N)
        store_result(prev, HALF, N)
        turn_result(prev - 1)
        round_result(nc.scalar.copy, prev, 0, 2)
        round_result(nc.scalar.copy, prev, 2, N_GROUPS)
        second_stage(last, 2, N_GROUPS, GPSIMD_RUNS_AT_END)
        turn_result(prev)
        for g in range(2, N_GROUPS):
            add_upper_offset(last, g * GROUP, (g + 1) * GROUP)
        store_result(last, 0, HALF)
        store_result(last, HALF, N)
        round_result(nc.scalar.copy, last, 0, 2)
        for g in range(2, N_GROUPS):
            round_result(nc.vector.tensor_copy, last, g, g + 1)
        turn_result_half(last, 1)
        turn_result_half(last, 0)
        quantize_result(prev - 1, all_groups)
        quantize_result(prev, all_groups)
        quantize_result(last, (2, 3, 0, 1))
